import numpy as np, ml_dtypes
CORES = [2,6,10,14,18,22,26,30]
N = 8
BF = ml_dtypes.bfloat16
def gentries(a):
    return np.ascontiguousarray(a.reshape(8, 16, -1).transpose(0, 2, 1)).reshape(8, -1)
def gtable(e):
    e = np.asarray(e); return np.ascontiguousarray(e.reshape(8, -1, 16).transpose(0, 2, 1)).reshape(128, -1).astype(np.int32)
U, D, RO, W = 512, 8, 3, 4096
def parts(rng):
    a = (rng.integers(32, 257, (N, 8, 1, U)) * rng.random((N, 8, 16, U))).astype(np.int64)
    s = rng.integers(0, W, (N, 8, D, U))
    w = np.where(rng.random((N, 8, 1, U)) < 0.5, rng.integers(-1, 2, s.shape), rng.integers(-3, 4, s.shape))
    return a, s, w, rng.integers(-300, 501, (N, 8, U))
def pack(a, s, w, b):
    return {"a0": np.ascontiguousarray(a.reshape(N, 128, U)).astype(np.float32).astype(BF), "sr": np.stack([gtable(x.reshape(8, D * U)) for x in s]),
            "wt": np.ascontiguousarray(w.reshape(N, 8, D * U)).astype(np.int32), "bs": np.ascontiguousarray(b).astype(np.int32)}
def setup_inputs(rng):
    return pack(*parts(rng))
def setup_inputs_ties(rng):
    a, s, w, b = parts(rng); a[..., 1::2] = a[..., ::2]
    m = rng.integers(0, 4, (N, 8, 1, U)); pick = rng.integers(0, 2, s.shape); x = s[:, :, :1]; y = s[:, :, 1:2]
    s = np.where(m == 0, x, np.where(m == 1, x ^ pick, np.where(m == 2, np.where(pick == 1, x, y), s)))
    w = np.where(m == 3, -np.abs(w), w); b = np.where(m[:, :, 0] == 3, -np.abs(b) - 1, np.abs(b))
    for v in (s, w, b): v[:, 4:, ..., 1::2] = v[:, 4:, ..., ::2]
    return pack(a, s, w, b)
def setup_inputs_ends(rng):
    a, s, w, b = parts(rng); own = np.arange(N).reshape(N, 1, 1) * U
    s[:, 0] = rng.choice(np.concatenate([np.arange(N) * U, np.arange(N) * U + U - 1]), (N, D, U))
    s[:, 1] = rng.choice(np.array([0, W - 1]), (N, D, U))
    s[:, 2] = own + rng.integers(0, U, (N, D, U))
    s[:, 3] = (own + U + rng.integers(0, W - U, (N, D, U))) & (W - 1)
    s[:, 4] = int(rng.integers(0, N)) * U + rng.integers(0, U, (N, D, U))
    s[:, 4, 0] = s[:, 4, 0] // U * U + np.arange(U)
    s[:, 5] = own + np.arange(U)
    s[:, 6] = np.argsort(rng.random((N, W)), axis=-1)[:, :D * U].reshape(N, D, U)
    return pack(a, s, w, b)
def setup_inputs_full(rng):
    a, s, w, b = parts(rng)
    a[:, 0] = rng.integers(254, 256, (N, 16, U)); a[:, 0] = np.where(rng.random((N, 1, U)) < 0.5, 255, a[:, 0]); a[:, 0, :, 0] = 255
    s[0, 0, :, 0] = 0; w[:, 0] = rng.integers(1, 4, (N, D, U)); b[:, 0] = 1000
    w[:, 1] = -3; b[:, 1] = -1000
    w[:, 2] = 0; b[:, 2] = rng.integers(240, 256, (N, U))
    w[:, 3] = 0; b[:, 3] = rng.choice(np.array([-1, 0, 1, 254, 255, 256]), (N, U))
    a[:, 4] = 255 * rng.integers(0, 2, (N, 16, U)); w[:, 4] = rng.choice(np.array([-3, 3]), (N, D, U)); b[:, 4] = rng.choice(np.array([-1000, 0, 1000]), (N, U))
    o = rng.permutation(16); x = int(rng.integers(200, 255)); h1 = np.zeros(16, np.int64)
    h1[o[0]] = x; h1[o[1]] = x + 1; h1[o[2:]] = 2 * rng.integers(95, 128, 14)
    h2 = h1.copy(); h2[o[0]] = x + 1; h2[o[1]] = x
    a[:, 5] = np.where(rng.integers(0, 2, (N, 1, U)) == 1, h1[:, None], h2[:, None])
    w[:, 5] = np.where(np.arange(D)[:, None] == rng.integers(0, D, (N, 1, U)), 1, 0); b[:, 5] = 0
    a[:, 6:] = rng.integers(0, 4, (N, 2, 16, U)) * (rng.random((N, 2, 16, U)) < 0.3)
    w[:, 6:] = rng.integers(-1, 2, (N, 2, D, U)); b[:, 6:] = rng.integers(-4, 9, (N, 2, U))
    return pack(a, s, w, b)
def setup_inputs_crowd(rng):
    a, s, w, b = parts(rng); a = np.maximum(a, 1); q = int(rng.integers(0, N))
    s = q * U + rng.integers(0, U, s.shape)
    live = [1, 3, 4, 5, 7]
    w[:, live] = rng.integers(1, 4, (N, 5, D, U)); b[:, live] = rng.integers(0, 101, (N, 5, U))
    w[:, 0:3:2] = -rng.integers(0, 4, (N, 2, D, U)); b[:, 0:3:2] = -1000
    u = q * U + np.arange(U); cand = u[(((20 * u) & (W - 1)) // U == q) & ((u & 1) == 1)]
    s[:, 1] = rng.choice(cand, (N, 1, 1)); s[:, 7] = rng.choice(cand, (N, 1, 1))
    for g, t in ((3, 1), (4, 2), (5, D - 1)):
        z = int(rng.integers(0, U)); a[q, g, :, z] = 0
        s[:, g] = q * U + ((z + 1 + rng.integers(0, U - 1, (N, D, U))) & (U - 1)); s[:, g, t] = q * U + z
    return pack(a, s, w, b)
def setup_inputs_spread(rng):
    a, s, w, b = parts(rng)
    a = np.minimum((np.exp2(8 * rng.random((N, 8, 1, U))) * rng.random(a.shape)).astype(np.int64) + 1, 255) * (rng.random((N, 8, 1, U)) > 0.0625)
    s = np.minimum((W * rng.random(s.shape) ** rng.integers(1, 5, (N, 8, 1, 1))).astype(np.int64), W - 1); s[:, 1::2] = W - 1 - s[:, 1::2]
    w = rng.integers(-3, 4, s.shape); b = rng.integers(-1000, 1001, b.shape)
    b[:, ::3] = (np.exp2(9.9 * rng.random((N, 3, U))) * rng.choice(np.array([-1, 1]), (N, 3, U))).astype(np.int64)
    return pack(a, s, w, b)
def check_inputs(d):
    bad = []; x = np.asarray(d["a0"]).astype(np.float32)
    if not np.all((x >= 0) & (x <= 255) & (x == np.floor(x))): bad.append("whole numbers from 0 to 255 in a0")
    for k, lo, hi in (("sr", 0, W - 1), ("wt", -3, 3), ("bs", -1000, 1000)):
        if np.min(d[k]) < lo or np.max(d[k]) > hi: bad.append("range of " + k)
    return bad
def reference(a0, sr, wt, bs):
    a = a0.astype(np.float32).astype(np.int64).reshape(N, 8, 16, U)
    s = np.stack([gentries(x) for x in sr]).astype(np.int64).reshape(N, 8, D, U)
    w = wt.astype(np.int64).reshape(N, 8, 1, D, U); b = bs.astype(np.int64).reshape(N, 8, 1, U)
    for rnd in range(RO):
        every = np.ascontiguousarray(a.transpose(1, 2, 0, 3)).reshape(8, 16, W)
        na, ns = [], []
        for r in range(N):
            p = np.take_along_axis(every, s[r].reshape(8, 1, D * U), 2).reshape(8, 16, D, U)
            v = np.minimum(np.maximum(b[r] + np.add.reduce(w[r] * p, axis=2), 0), 255)
            c = np.add.reduce(p * v[:, :, None, :], axis=1)
            best = np.argmax(c, axis=1)[:, None, :]; worst = np.argmin(c, axis=1)[:, None, :]
            top = np.roll(np.take_along_axis(c, best, 1), -1, axis=0)
            new = (13 * np.take_along_axis(s[r], best, 1) + 7 * np.take_along_axis(s[r], worst, 1) + top) & (W - 1)
            na.append(v); ns.append(np.where(np.arange(D)[None, :, None] == worst, new, s[r]))
        a = np.stack(na); s = np.stack(ns)
    return {"ya": a.reshape(N, 128, U).astype(np.float32).astype(BF), "ys": np.stack([gtable(x.reshape(8, D * U)) for x in s]).astype(np.float32)}

@@ -1,0 +1,491 @@
+from concourse.bass import DstId, RemoteDMATransfer
+from concourse.mybir import AluOpType, ActivationFunctionType
+
+RO = 3
+OPT = {
+    "clamp_s": (1,),
+    "forward": ((True, False), (True, False), (True, False)),
+}
+
+SCRATCH = {
+    "tab0": ("sbuf", [128, 4096], "bfloat16"), "tab1": ("sbuf", [128, 4096], "bfloat16"),
+    "tab2": ("sbuf", [128, 4096], "bfloat16"), "aout": ("sbuf", [128, 512], "bfloat16"),
+    "p": ("sbuf", [128, 4096], "bfloat16"), "wp": ("sbuf", [128, 4096], "float16"),
+    "q": ("sbuf", [128, 4096], "float32"), "wsb": ("sbuf", [128, 2048], "bfloat16"),
+    "off": ("sbuf", [128, 256], "uint16"),
+    "sri": ("sbuf", [128, 256], "int32"), "wti": ("sbuf", [128, 256], "int32"), "bsi": ("sbuf", [128, 512], "int32"),
+    "wtb": ("sbuf", [128, 256], "bfloat16"), "bsh": ("sbuf", [128, 512], "float16"),
+    "kc": ("sbuf", [128, 16], "float32"), "n128": ("sbuf", [128, 128], "bfloat16"),
+    "m16": ("sbuf", [128, 128], "bfloat16"), "lf": ("sbuf", [128, 64], "float32"),
+    "en": ("sbuf", [128, 256], "bfloat16"), "em": ("sbuf", [128, 512], "float16"),
+    "zh": ("sbuf", [128, 256], "float16"), "neg": ("sbuf", [128, 512], "bfloat16"),
+    "ki": ("sbuf", [128, 16], "int32"), "kj": ("sbuf", [128, 8], "int32"),
+    "rf": ("sbuf", [128, 8], "float32"), "rs": ("sbuf", [128, 8], "float32"),
+    "lst": ("sbuf", [128, 64], "uint16"),
+    "sel": ("sbuf", [128, 2048], "bfloat16"),
+    "idf": ("sbuf", [128, 128], "float32"), "idn": ("sbuf", [128, 128], "float32"),
+    "idb": ("sbuf", [128, 128], "bfloat16"), "idh": ("sbuf", [128, 128], "float16"),
+    "e8": ("sbuf", [128, 128], "float16"), "grp": ("sbuf", [128, 16], "float32"),
+    "one": ("sbuf", [128, 128], "bfloat16"), "tie": ("sbuf", [128, 512], "bfloat16"),
+    "d1": ("sbuf", [128, 512], "bfloat16"), "d2": ("sbuf", [128, 512], "bfloat16"),
+    "z0": ("sbuf", [128, 256], "float32"), "z1": ("sbuf", [128, 256], "float32"),
+    "z2": ("sbuf", [128, 256], "float32"),
+    "src": ("sbuf", [128, 256], "float32"), "mx": ("sbuf", [128, 512], "float32"),
+    "oh": ("sbuf", [128, 512], "float32"), "pay": ("sbuf", [128, 512], "float32"),
+    "sc": ("sbuf", [128, 512], "float32"), "kn": ("sbuf", [128, 32], "float32"),
+    "za": ("sbuf", [128, 32], "float32"), "zb": ("sbuf", [128, 32], "float32"),
+    "zi": ("sbuf", [128, 32], "int32"), "nw": ("sbuf", [128, 32], "int32"),
+    "nd": ("sbuf", [128, 32], "float32"), "nu": ("sbuf", [128, 256], "float32"),
+    "pw0": ("psum", [128, 512], "float32"), "pw1": ("psum", [128, 512], "float32"),
+    "pw2": ("psum", [128, 512], "float32"), "pw3": ("psum", [128, 512], "float32"),
+    "px0": ("psum", [128, 512], "float32"), "px1": ("psum", [128, 512], "float32"),
+    "pk": ("psum", [128, 512], "float32"), "ps": ("psum", [128, 512], "float32"),
+}
+SEMAPHORES = (["cv", "cs", "ct", "cg", "sent", "la0", "la1", "lsr", "lwt", "lbs", "oy0", "oy1", "oys"]
+              + ["far%d%d" % (r, h) for r in range(RO) for h in range(2)] + ["near%d" % r for r in range(RO)])
+
+A = AluOpType
+COPY = ActivationFunctionType.Copy
+IDENT = ActivationFunctionType.Identity
+RELU = ActivationFunctionType.Relu
+
+
+def rank_program(g, core, T, topo):
+    rank = T.rank_of(core)
+    if rank is None:
+        return
+    queue = {"v": g.vector, "s": g.scalar, "t": g.tensor, "g": g, "y": g.sync}
+    own_sem = {"v": "cv", "s": "cs", "t": "ct", "g": "cg"}
+    ops = []
+    fwd = OPT["forward"]
+    clamp_s = OPT["clamp_s"]
+
+    def w(name, a=0, b=None, st=1, rows=128):
+        if b is None:
+            b = SCRATCH[name][1][1]
+        bits = 0
+        if st == 1:
+            bits = ((1 << (b - a)) - 1) << a
+            ap = T[name][0:rows, a:b]
+        else:
+            for c in range(a, b, st):
+                bits |= 1 << c
+            ap = T[name][0:rows, a:b:st]
+        return (name, ap, bits)
+
+    def ind(win, lst):
+        return ("", win[1].indirect(lst[1]), 0, [win, lst])
+
+    def parts(x):
+        if not isinstance(x, tuple):
+            return []
+        return x[3] if len(x) == 4 else [x]
+
+    def val(x):
+        return x[1] if isinstance(x, tuple) else x
+
+    def op(q, fn, reads, writes, ext=(), dma=None, mute=False):
+        rd = []
+        for x in reads:
+            rd += parts(x)
+        ops.append({"q": q, "fn": fn, "r": rd, "w": list(writes), "ext": list(ext), "dma": dma, "mute": mute})
+
+    def tt(out, a, b, f, ext=()):
+        op("v", lambda: g.vector.tensor_tensor(out[1], a[1], b[1], f), [a, b], [out], ext)
+
+    def ts(out, a, s1, s2, f0, f1=None):
+        if f1 is None:
+            op("v", lambda: g.vector.tensor_scalar(out[1], a[1], val(s1), None, f0), [a, s1], [out])
+        else:
+            op("v", lambda: g.vector.tensor_scalar(out[1], a[1], val(s1), val(s2), f0, f1), [a, s1, s2], [out])
+
+    def cp(out, a):
+        op("v", lambda: g.vector.tensor_copy(out[1], a[1]), [a], [out])
+
+    def fill(out, c):
+        op("v", lambda: g.vector.memset(out[1], c), [], [out])
+
+    def scan(out, a, b, f0, f1):
+        op("v", lambda: g.vector.tensor_tensor_scan(out[1], a[1], b[1], 0.0, f0, f1), [a, b], [out])
+
+    def turn(out, a):
+        op("v", lambda: g.vector.transpose(out[1], a[1]), [a], [out])
+
+    def act(out, a, scale=1.0, ext=(), f=COPY, bias=0.0):
+        op("s", lambda: g.scalar.activation(out[1], a[1], f, bias=bias, scale=scale), [a], [out], ext)
+
+    def mm(out, l, r, start=True, stop=True):
+        op("t", lambda: g.tensor.matmul(out[1], l[1], r[1], start, stop), [l, r], [out])
+
+    def iota(out, pat, base, cm):
+        op("g", lambda: g.iota(out[1], pat, base, cm, allow_small_or_imprecise_dtypes=True), [], [out])
+
+    def load(q, out, src, sem):
+        op(q, lambda: queue[q].dma_start(out[1], src), [], [out], dma=sem)
+
+    def store(q, dst, a, sem):
+        op(q, lambda: queue[q].dma_start(dst, a[1]), [a], [], dma=sem)
+
+    cores = list(T.cores)
+    near = [c for c in cores if c != core and topo.chip(c) == topo.chip(core)][0]
+    far = [c for c in cores if topo.chip(c) != topo.chip(core)]
+    far_die = [c for c in far if topo.die(c) == topo.die(core)]
+    e_far = topo.engines(core, far[0])
+    e_near = [e for e in topo.engines(core, near) if e not in e_far]
+    half = len(e_near) // 2
+    sent = [0]
+
+    def mask(es):
+        m = 0
+        for e in es:
+            m |= 1 << e
+        return m
+
+    def dst(c):
+        rid, pid, _ = topo.addr(c)
+        return DstId(rid=rid, pnc=pid)
+
+    def block(r, c, h):
+        a = T.rank_of(c) * 512 + h * 256
+        return w("tab%d" % r, a, a + 256)
+
+    hand_on = [[(far_die[0], e_near[:half]), (far_die[1], e_near[half:])], [(far_die[2], e_near)]]
+
+    def far_count(r, h):
+        return len(e_far) * len(far_die if fwd[r][h] else far)
+
+    def near_count(r):
+        return ((1 if r == 0 else 2) + 2 * sum(fwd[r])) * len(e_near)
+
+    def send(r, b, h, to_far=True, to_near=True):
+        to = far_die if fwd[r][h] else far
+        tr = []
+        if to_far:
+            tr.append(RemoteDMATransfer(dst_ids=[dst(c) for c in to], dma_engine_mask=mask(e_far),
+                                        remote_sem=T.sem["far%d%d" % (r, h)], srcs=[b[1]], dsts=[b[1] for c in to]))
+            sent[0] += len(e_far)
+        if to_near:
+            tr.append(RemoteDMATransfer(dst_ids=[dst(near)], dma_engine_mask=mask(e_near),
+                                        remote_sem=T.sem["near%d" % r], srcs=[b[1]], dsts=[b[1]]))
+            sent[0] += len(e_near)
+        op("g", lambda: g.remote_dma_fused(tr, local_sem=T.sem.sent), [b], [], mute=True)
+
+    def forward_call(r, h, call):
+        tr = []
+        for c, es in call:
+            b = block(r, c, h)
+            tr.append(RemoteDMATransfer(dst_ids=[dst(near)], dma_engine_mask=mask(es),
+                                        remote_sem=T.sem["near%d" % r], srcs=[b[1]], dsts=[b[1]]))
+            sent[0] += len(es)
+        op("g", lambda: g.remote_dma_fused(tr, local_sem=T.sem.sent), [], [],
+           ext=[("far%d%d" % (r, h), far_count(r, h))], mute=True)
+
+    def forward(r):
+        for h in range(2):
+            if fwd[r][h]:
+                for call in hand_on:
+                    forward_call(r, h, call)
+
+    def landed(r):
+        return [("far%d0" % r, far_count(r, 0)), ("far%d1" % r, far_count(r, 1)), ("near%d" % r, near_count(r))]
+
+    px = ["px0", "px1"]
+    L_A, L_B, L_F, L_BC, L_T, L_S, L_K = 0, 16, 32, 48, 56, 58, 60
+
+    load("y", block(0, core, 0), T.a0[:, 0:256], "la0")
+    load("s", block(0, core, 1), T.a0[:, 256:512], "la1")
+    load("y", w("sri"), T.sr[:, :], "lsr")
+    load("s", w("wti"), T.wt[:, :], "lwt")
+    load("y", w("bsi", rows=8), T.bs[:, :], "lbs")
+
+    iota(w("kc"), [[-1, 16]], 0, 1)
+    iota(w("m16"), [[16, 8], [0, 16]], 0, 0)
+    iota(w("lf", L_A, L_A + 16), [[1, 8], [16, 2]], 0, 0)
+    iota(w("lf", L_B, L_B + 16), [[16, 2], [32, 8]], 0, 0)
+    iota(w("n128"), [[1, 128]], 0, 0)
+    send(0, block(0, core, 0), 0, to_near=False)
+    send(0, block(0, core, 1), 1, to_near=False)
+    send(0, w("tab0", rank * 512, rank * 512 + 512), 0, to_far=False)
+    iota(w("lf", L_F, L_F + 16), [[16, 2], [32, 4], [128, 2]], 0, 0)
+    iota(w("lf", L_BC, L_BC + 8), [[2, 8]], 0, 0)
+    iota(w("lf", L_T, L_T + 4), [[128, 2], [256, 2]], 7, 0)
+    forward(0)
+    iota(w("en"), [[16, 8], [128, 2], [1, 16]], 0, 0)
+
+    fill(w("one", rows=32), 1.0)
+    fill(w("d1"), 0.0)
+    for s in range(8):
+        act(w("tie", s, 512, 8, rows=1), w("one", 0, 64, rows=1), scale=float(7 - s))
+    k = w("kc", 0, 1)
+    cp(w("ki"), w("kc"))
+
+    def sel(t0, t1):
+        for t in range(t0, t1):
+            ts(w("sel", t * 128, t * 128 + 128), w("m16"), w("kc", t, t + 1), None, A.is_equal)
+
+    fill(w("d1", 0, 512, 8), -3.0e7)
+    ts(w("kj", 0, 1), w("ki", 0, 1), 15, None, A.bitwise_and)
+    ts(w("kj", 1, 2), w("ki", 0, 1), 3, 1, A.arith_shift_right, A.bitwise_and)
+    ts(w("kj", 2, 3), w("ki", 0, 1), 7, None, A.bitwise_and)
+    ts(w("kj", 3, 4), w("ki", 0, 1), 4, None, A.arith_shift_right)
+    ts(w("kj", 4, 5), w("ki", 14, 15), 15, None, A.bitwise_and)
+    sel(0, 2)
+    cp(w("rf", 0, 5), w("kj", 0, 5))
+    sel(2, 4)
+    ts(w("rs", 0, 5), w("rf", 0, 5), 8.0, None, A.mult)
+    ts(w("rs", 5, 6), w("rf", 2, 3), 32.0, None, A.mult)
+    sel(4, 8)
+    ts(w("lst", L_A, L_A + 16), w("lf", L_A, L_A + 16), w("rs", 1, 2), w("rs", 5, 6), A.add, A.add)
+    ts(w("lst", L_B, L_B + 16), w("lf", L_B, L_B + 16), w("rf", 0, 1), None, A.add)
+    ts(w("idb"), w("n128"), k, None, A.is_equal)
+    ts(w("idh"), w("n128"), k, None, A.is_equal)
+    act(w("idf"), w("idb"))
+    act(w("idn"), w("idb"), scale=-1.0)
+    sel(8, 16)
+
+    def weights(bank, chunk):
+        h, c = chunk // 4, chunk % 4
+        for s in range(8):
+            t = 2 * s + h
+            mm(w(bank, s, 512, 8), w("sel", t * 128, t * 128 + 128), w("wtb", c * 64, c * 64 + 64))
+
+    cp(w("z0"), ind(w("sri"), w("lst", L_A, L_A + 16)))
+    for b in range(2):
+        cp(w("wtb", b, 256, 2), w("wti", b * 128, b * 128 + 128))
+    weights("px0", 0)
+    weights("px1", 1)
+    turn(w("z1"), w("z0"))
+    ts(w("e8", rows=8), w("m16", rows=8), 0.0625, w("kc", 0, 1, rows=8), A.mult, A.is_equal)
+    ts(w("zh"), ind(w("z1"), w("lst", L_B, L_B + 16)), -2048.0, None, A.add)
+    for g0 in range(2):
+        for g21 in range(4):
+            for h in range(2):
+                a = h * 128 + (g21 * 2 + g0) * 16
+                n = g21 * 32 + h * 16
+                mm(w("pk", a, a + 16), w("zh", g0 * 128, g0 * 128 + 128), w("idh", n, n + 16))
+    cp(w("bsh", rows=8), w("bsi", rows=8))
+    weights("pw2", 6)
+    ts(w("src"), w("pk", 0, 256), 2048.0, None, A.add)
+    for h in range(2):
+        mm(w("pk", h * 128, h * 128 + 128), w("src", h * 128, h * 128 + 128), w("idf"))
+    weights("pw3", 7)
+    weights("pw0", 2)
+    weights("pw1", 3)
+    act(w("wsb", 0, 512), w("px0"))
+    act(w("wsb", 512, 1024), w("px1"))
+    act(w("wsb", 1024, 1536), w("pw2"))
+    act(w("wsb", 1536, 2048), w("pw3"))
+    weights("pw2", 4)
+    weights("pw3", 5)
+    fill(w("d2"), 1.0)
+    ts(w("grp", 0, 8), w("n128", 0, 8), w("rf", 3, 4), -8.0, A.is_equal, A.mult)
+    ts(w("grp", 8, 16), w("n128", 0, 8), w("rf", 3, 4), 8.0, A.is_equal, A.mult)
+    ts(w("rs", 6, 7), k, 128.0, None, A.add)
+    fill(w("d2", 0, 512, 8), 0.0)
+    cp(w("off"), w("pk", 0, 256))
+    ts(w("lst", L_F, L_F + 16), w("lf", L_F, L_F + 16), w("rf", 0, 1), None, A.add)
+    ts(w("lst", L_BC, L_BC + 8), w("lf", L_BC, L_BC + 8), w("rf", 1, 2), None, A.add)
+    ts(w("lst", L_T, L_T + 4), w("lf", L_T, L_T + 4), w("rs", 0, 1), None, A.add)
+    ts(w("lst", L_K, L_K + 2), w("lf", L_S, L_S + 2), w("rs", 4, 5), None, A.add)
+
+    for r in range(RO):
+        last = r == RO - 1
+        tab = w("tab%d" % r)
+        arrived = landed(r)
+
+        def new_a(h, a=0, b=256):
+            if last:
+                return w("aout", h * 256 + a, h * 256 + b)
+            return w("tab%d" % (r + 1), rank * 512 + h * 256 + a, rank * 512 + h * 256 + b)
+
+        def gather(c0, c1):
+            act(w("p", c0 * 512, c1 * 512), ind(tab, w("off", c0 * 32, c1 * 32)), ext=arrived)
+
+        def gather_mul(c0, c1):
+            a = c0 * 512 if c0 < 4 else (c0 - 4) * 512
+            tt(w("wp", c0 * 512, c1 * 512), ind(tab, w("off", c0 * 32, c1 * 32)),
+               w("wsb", a, a + (c1 - c0) * 512), A.mult, ext=arrived)
+
+        def mul(c):
+            tt(w("wp", c * 512, c * 512 + 512), w("p", c * 512, c * 512 + 512), w("pw%d" % (c - 2)), A.mult)
+
+        def bias(h):
+            mm(w(px[h], 0, 256), w("e8", rows=8), w("bsh", h * 256, h * 256 + 256, rows=8), True, False)
+
+        def wires(qt, stop):
+            h, mh = qt // 2, qt % 2
+            for b in range(2):
+                for s in range(8):
+                    a = b * 128 + mh * 64
+                    mm(w(px[h], a, a + 64), w("idh"), w("wp", qt * 1024 + b * 8 + s, qt * 1024 + 1024, 16),
+                       False, stop and b == 1 and s == 7)
+
+        def clamp(h):
+            if h in clamp_s:
+                act(w("neg", h * 256, h * 256 + 256), w(px[h], 0, 256), -1.0, f=RELU, bias=255.0)
+                act(new_a(h), w("neg", h * 256, h * 256 + 256), -1.0, f=RELU, bias=255.0)
+            else:
+                ts(new_a(h), w(px[h], 0, 256), 0.0, 255.0, A.max, A.min)
+            if last:
+                store("y", T.ya[:, h * 256:h * 256 + 256], new_a(h), "oy%d" % h)
+            else:
+                send(r + 1, new_a(h), h)
+
+        def spread(h):
+            for b in range(2):
+                mm(w(px[h], 256 + b, 512, 2), w("idb"), new_a(h, b * 128, b * 128 + 128))
+
+        def score_mul(h, s):
+            a = (h * 8 + s) * 256
+            tt(w("q", a, a + 256), w("p", h * 2048 + s, h * 2048 + 2048, 8), w(px[h], 256, 512), A.mult)
+
+        def score_sum(h, s):
+            a = (h * 8 + s) * 256
+            for b in range(2):
+                mm(w("pk", h * 256 + b * 8 + s, h * 256 + 256, 16), w("q", a + b, a + 256, 2), w("grp"),
+                   False, h == 1 and s == 7 and b == 1)
+
+        def score(h, s):
+            score_mul(h, s)
+            score_sum(h, s)
+
+        def renew(h):
+            tt(w("src", h * 128, h * 128 + 128), w("ps", h * 256, h * 256 + 128),
+               w("nu", h * 128, h * 128 + 128), A.subtract)
+
+        bias(0)
+        bias(1)
+        mm(w("pk"), w("one", rows=1), w("tie", rows=1), True, False)
+        gather(2, 3)
+        gather_mul(0, 2)
+        gather(3, 4)
+        wires(0, False)
+        gather(4, 5)
+        mul(2)
+        mul(3)
+        gather(5, 6)
+        wires(1, True)
+        gather_mul(6, 7)
+        if 0 not in clamp_s:
+            gather(0, 2)
+        clamp(0)
+        if 0 in clamp_s:
+            gather(0, 2)
+        spread(0)
+        gather_mul(7, 8)
+        wires(3, False)
+        mul(4)
+        mul(5)
+        wires(2, True)
+        gather(6, 7)
+        score(0, 0)
+        score(0, 1)
+        clamp(1)
+        gather(7, 8)
+        if not last:
+            forward(r + 1)
+        for s in range(2, 8):
+            score(0, s)
+            if s == 5:
+                spread(1)
+        for s in range(8):
+            score(1, s)
+        if r:
+            renew(1)
+        else:
+            for h in range(2):
+                ts(w("em", h * 256, h * 256 + 256), w("en"), w("rs", 6, 7) if h else k, -1.0, A.is_equal, A.mult)
+        for h in range(2):
+            act(w("ps", h * 256, h * 256 + 128), w("src", h * 128, h * 128 + 128))
+            act(w("ps", h * 256 + 128, h * 256 + 256), w("src", h * 128, h * 128 + 128), scale=104.0)
+        if not last:
+            for h in range(2):
+                mm(w(px[h], 0, 128), w("src", h * 128, h * 128 + 128), w("idf"), True, False)
+
+        scan(w("mx"), w("d1"), w("pk"), A.add, A.max)
+        for s in range(8):
+            tt(w("oh", s, 512, 8), w("pk", s, 512, 8), w("mx", 7, 512, 8), A.is_equal)
+        act(w("kn"), ind(w("mx"), w("lst", L_K, L_K + 2)))
+        if last:
+            act(w("z0"), ind(w("src"), w("lst", L_F, L_F + 16)), f=IDENT, bias=-2048.0)
+        tt(w("pay"), w("oh"), w("ps"), A.mult)
+        scan(w("sc"), w("d2"), w("pay"), A.mult, A.add)
+        tt(w("za"), ind(w("sc"), w("lst", L_S, L_S + 2)), w("kn"), A.add)
+        act(w("zb"), ind(w("sc"), w("lst", L_T, L_T + 2)), scale=56.0)
+        tt(w("zi"), w("za"), w("zb"), A.add)
+        ts(w("nw"), w("zi"), 3, 4095, A.arith_shift_right, A.bitwise_and)
+        tt(w("nd"), ind(w("sc"), w("lst", L_T, L_T + 2)), w("nw"), A.subtract)
+        for h in range(2):
+            tt(w("nu", h * 128, h * 128 + 128), ind(w("nd", h * 16, h * 16 + 16), w("lst", L_BC, L_BC + 8)),
+               w("oh", h * 256, h * 256 + 128), A.mult)
+            if not last:
+                mm(w(px[h], 0, 128), w("nu", h * 128, h * 128 + 128), w("idn"), False, True)
+        if not last:
+            renew(0)
+            for h in range(2):
+                cp(w("off", h * 128, h * 128 + 128), w(px[h], 0, 128))
+        else:
+            tt(w("zh"), ind(w("nu"), w("lst", L_F, L_F + 16)), w("z0"), A.subtract)
+            for g0 in range(2):
+                mm(w("pk", 0, 256), w("zh", g0 * 128, g0 * 128 + 128), w("em", g0 * 256, g0 * 256 + 256),
+                   g0 == 0, g0 == 1)
+            turn(w("z2"), w("pk", 0, 256))
+            ts(w("z0"), ind(w("z2"), w("lst", L_A, L_A + 16)), 2048.0, None, A.add)
+            store("y", T.ys[:, :], w("z0"), "oys")
+
+    def psum(name):
+        return SCRATCH[name][0] == "psum"
+
+    history = {}
+    for n, o in enumerate(ops):
+        deps = set()
+        for views, writing in ((o["r"], False), (o["w"], True)):
+            for name, _, bits in views:
+                seen = set()
+                for m, mq, mbits, mw in reversed(history.get(name, [])):
+                    if mq == o["q"] and ops[m]["dma"] is None:
+                        hit = mq != "t" and (mbits & bits) and (mw or writing)
+                    else:
+                        hit = psum(name) or ((mbits & bits) and (mw or writing))
+                    key = ops[m]["dma"] or mq
+                    if hit and not ops[m]["mute"] and key not in seen:
+                        seen.add(key)
+                        deps.add(m)
+        o["deps"] = deps
+        for views, writing in ((o["r"], False), (o["w"], True)):
+            for name, _, bits in views:
+                history.setdefault(name, []).append((n, o["q"], bits, writing))
+
+    known = {q: {} for q in queue}
+    for n, o in enumerate(ops):
+        need = {}
+        for m in o["deps"]:
+            key = ops[m]["dma"] or ops[m]["q"]
+            if known[o["q"]].get(key, -1) < m:
+                need[key] = max(need.get(key, -1), m)
+        for key, m in need.items():
+            known[o["q"]][key] = m
+            ops[m]["signal"] = True
+        o["need"] = sorted(need.values())
+
+    count = {q: 0 for q in queue}
+    waited = {q: set() for q in queue}
+    for o in ops:
+        q = o["q"]
+        for m in o["need"]:
+            queue[q].wait_ge(T.sem[ops[m]["token"][0]], ops[m]["token"][1])
+        for e in o["ext"]:
+            if e not in waited[q]:
+                waited[q].add(e)
+                queue[q].wait_ge(T.sem[e[0]], e[1])
+        ins = o["fn"]()
+        if o["dma"]:
+            ins.then_inc(T.sem[o["dma"]], 16)
+            o["token"] = (o["dma"], 16)
+        elif o.get("signal"):
+            count[q] += 1
+            ins.then_inc(T.sem[own_sem[q]], 1)
+            o["token"] = (own_sem[q], count[q])
+    g.wait_ge(T.sem.sent, sent[0])
+    for name in ("oy0", "oy1", "oys"):
+        g.sync.wait_ge(T.sem[name], 16)

@@ -3,43 +3,43 @@ from concourse.mybir import AluOpType, ActivationFunctionType
 
 RO = 3
 OPT = {
-    "clamp_s": (1,),
-    "forward": ((True, False), (True, False), (True, False)),
+    "forward": ((True, True), (True, True), (True, True)),
 }
+PAD = 272
+RESIDENT = {1: "pw0", 2: "pw1"}
+IN_SBUF = {0: 0, 4: 1, 3: 2, 5: 3, 6: 4, 7: 5}
 
 SCRATCH = {
     "tab0": ("sbuf", [128, 4096], "bfloat16"), "tab1": ("sbuf", [128, 4096], "bfloat16"),
     "tab2": ("sbuf", [128, 4096], "bfloat16"), "aout": ("sbuf", [128, 512], "bfloat16"),
     "p": ("sbuf", [128, 4096], "bfloat16"), "wp": ("sbuf", [128, 4096], "float16"),
-    "q": ("sbuf", [128, 4096], "float32"), "wsb": ("sbuf", [128, 2048], "bfloat16"),
+    "q": ("sbuf", [128, 4096], "float32"), "wsb": ("sbuf", [128, 3584], "bfloat16"),
     "off": ("sbuf", [128, 256], "uint16"),
     "sri": ("sbuf", [128, 256], "int32"), "wti": ("sbuf", [128, 256], "int32"), "bsi": ("sbuf", [128, 512], "int32"),
     "wtb": ("sbuf", [128, 256], "bfloat16"), "bsh": ("sbuf", [128, 512], "float16"),
     "kc": ("sbuf", [128, 16], "float32"), "n128": ("sbuf", [128, 128], "bfloat16"),
-    "m16": ("sbuf", [128, 128], "bfloat16"), "lf": ("sbuf", [128, 64], "float32"),
-    "en": ("sbuf", [128, 256], "bfloat16"), "em": ("sbuf", [128, 512], "float16"),
+    "m16": ("sbuf", [128, 128], "bfloat16"), "lf": ("sbuf", [128, 32], "float32"),
     "zh": ("sbuf", [128, 256], "float16"), "neg": ("sbuf", [128, 512], "bfloat16"),
     "ki": ("sbuf", [128, 16], "int32"), "kj": ("sbuf", [128, 8], "int32"),
     "rf": ("sbuf", [128, 8], "float32"), "rs": ("sbuf", [128, 8], "float32"),
-    "lst": ("sbuf", [128, 64], "uint16"),
-    "sel": ("sbuf", [128, 2048], "bfloat16"),
-    "idf": ("sbuf", [128, 128], "float32"), "idn": ("sbuf", [128, 128], "float32"),
+    "lst": ("sbuf", [128, 32], "uint16"),
+    "sel": ("sbuf", [128, 2048], "bfloat16"), "mov": ("sbuf", [128, 512], "float16"),
+    "idf": ("sbuf", [128, 512], "float32"),
     "idb": ("sbuf", [128, 128], "bfloat16"), "idh": ("sbuf", [128, 128], "float16"),
+    "idn": ("sbuf", [128, 128], "float16"),
     "e8": ("sbuf", [128, 128], "float16"), "grp": ("sbuf", [128, 16], "float32"),
-    "one": ("sbuf", [128, 128], "bfloat16"), "tie": ("sbuf", [128, 512], "bfloat16"),
-    "d1": ("sbuf", [128, 512], "bfloat16"), "d2": ("sbuf", [128, 512], "bfloat16"),
+    "one": ("sbuf", [128, 128], "bfloat16"), "tie": ("sbuf", [128, 256], "bfloat16"),
+    "src": ("sbuf", [128, 256], "float32"), "seed": ("sbuf", [128, 128], "bfloat16"), "mid": ("sbuf", [128, 256], "bfloat16"),
+    "d1": ("sbuf", [128, 256], "bfloat16"),
     "z0": ("sbuf", [128, 256], "float32"), "z1": ("sbuf", [128, 256], "float32"),
-    "z2": ("sbuf", [128, 256], "float32"),
-    "src": ("sbuf", [128, 256], "float32"), "mx": ("sbuf", [128, 512], "float32"),
-    "oh": ("sbuf", [128, 512], "float32"), "pay": ("sbuf", [128, 512], "float32"),
-    "sc": ("sbuf", [128, 512], "float32"), "kn": ("sbuf", [128, 32], "float32"),
-    "za": ("sbuf", [128, 32], "float32"), "zb": ("sbuf", [128, 32], "float32"),
-    "zi": ("sbuf", [128, 32], "int32"), "nw": ("sbuf", [128, 32], "int32"),
-    "nd": ("sbuf", [128, 32], "float32"), "nu": ("sbuf", [128, 256], "float32"),
+    "mx": ("sbuf", [128, 512], "float32"), "nq": ("sbuf", [128, 512], "float16"),
+    "sc": ("sbuf", [128, 512], "float32"),
+    "zi": ("sbuf", [128, 64], "int32"), "nw": ("sbuf", [128, 64], "int32"),
+    "inj": ("sbuf", [128, 512], "float16"), "dd": ("sbuf", [128, 2 * PAD], "float16"),
     "pw0": ("psum", [128, 512], "float32"), "pw1": ("psum", [128, 512], "float32"),
-    "pw2": ("psum", [128, 512], "float32"), "pw3": ("psum", [128, 512], "float32"),
     "px0": ("psum", [128, 512], "float32"), "px1": ("psum", [128, 512], "float32"),
-    "pk": ("psum", [128, 512], "float32"), "ps": ("psum", [128, 512], "float32"),
+    "pk0": ("psum", [128, 512], "float32"), "pk1": ("psum", [128, 512], "float32"),
+    "lu0": ("psum", [128, 512], "float32"), "lu1": ("psum", [128, 512], "float32"),
 }
 SEMAPHORES = (["cv", "cs", "ct", "cg", "sent", "la0", "la1", "lsr", "lwt", "lbs", "oy0", "oy1", "oys"]
               + ["far%d%d" % (r, h) for r in range(RO) for h in range(2)] + ["near%d" % r for r in range(RO)])
@@ -58,7 +58,6 @@ def rank_program(g, core, T, topo):
     own_sem = {"v": "cv", "s": "cs", "t": "ct", "g": "cg"}
     ops = []
     fwd = OPT["forward"]
-    clamp_s = OPT["clamp_s"]
 
     def w(name, a=0, b=None, st=1, rows=128):
         if b is None:
@@ -67,6 +66,9 @@ def rank_program(g, core, T, topo):
         if st == 1:
             bits = ((1 << (b - a)) - 1) << a
             ap = T[name][0:rows, a:b]
+        elif st == -1:
+            bits = ((1 << (b - a)) - 1) << a
+            ap = T[name][0:rows, b - 1:a - 1:-1] if a else T[name][0:rows, b - 1::-1]
         else:
             for c in range(a, b, st):
                 bits |= 1 << c
@@ -189,8 +191,8 @@ def rank_program(g, core, T, topo):
     def landed(r):
         return [("far%d0" % r, far_count(r, 0)), ("far%d1" % r, far_count(r, 1)), ("near%d" % r, near_count(r))]
 
-    px = ["px0", "px1"]
-    L_A, L_B, L_F, L_BC, L_T, L_S, L_K = 0, 16, 32, 48, 56, 58, 60
+    px, pk, lu = ["px0", "px1"], ["pk0", "pk1"], ["lu0", "lu1"]
+    L_A, L_B = 0, 16
 
     load("y", block(0, core, 0), T.a0[:, 0:256], "la0")
     load("s", block(0, core, 1), T.a0[:, 256:512], "la1")
@@ -206,16 +208,14 @@ def rank_program(g, core, T, topo):
     send(0, block(0, core, 0), 0, to_near=False)
     send(0, block(0, core, 1), 1, to_near=False)
     send(0, w("tab0", rank * 512, rank * 512 + 512), 0, to_far=False)
-    iota(w("lf", L_F, L_F + 16), [[16, 2], [32, 4], [128, 2]], 0, 0)
-    iota(w("lf", L_BC, L_BC + 8), [[2, 8]], 0, 0)
-    iota(w("lf", L_T, L_T + 4), [[128, 2], [256, 2]], 7, 0)
     forward(0)
-    iota(w("en"), [[16, 8], [128, 2], [1, 16]], 0, 0)
 
     fill(w("one", rows=32), 1.0)
     fill(w("d1"), 0.0)
     for s in range(8):
-        act(w("tie", s, 512, 8, rows=1), w("one", 0, 64, rows=1), scale=float(7 - s))
+        act(w("tie", s, 256, 8, rows=1), w("one", 0, 32, rows=1), scale=float(7 - s))
+    act(w("seed", rows=1), w("tie", 0, 128, rows=1), scale=4096.0, f=IDENT, bias=2048.0)
+    act(w("mid", rows=1), w("tie", rows=1), scale=0.0, f=IDENT, bias=2048.0)
     k = w("kc", 0, 1)
     cp(w("ki"), w("kc"))
 
@@ -223,25 +223,44 @@ def rank_program(g, core, T, topo):
         for t in range(t0, t1):
             ts(w("sel", t * 128, t * 128 + 128), w("m16"), w("kc", t, t + 1), None, A.is_equal)
 
-    fill(w("d1", 0, 512, 8), -3.0e7)
+    def mov(to, frm):
+        a = (to * 2 + frm) * 128
+        return w("mov", a, a + 128)
+
+    def idf(n):
+        return w("idf", n * 128, n * 128 + 128)
+
+    fill(w("d1", 0, 256, 8), -3.0e7)
     ts(w("kj", 0, 1), w("ki", 0, 1), 15, None, A.bitwise_and)
     ts(w("kj", 1, 2), w("ki", 0, 1), 3, 1, A.arith_shift_right, A.bitwise_and)
     ts(w("kj", 2, 3), w("ki", 0, 1), 7, None, A.bitwise_and)
     ts(w("kj", 3, 4), w("ki", 0, 1), 4, None, A.arith_shift_right)
-    ts(w("kj", 4, 5), w("ki", 14, 15), 15, None, A.bitwise_and)
+    ts(w("kj", 4, 5), w("ki", 0, 1), 4, 1, A.arith_shift_right, A.bitwise_and)
     sel(0, 2)
     cp(w("rf", 0, 5), w("kj", 0, 5))
     sel(2, 4)
-    ts(w("rs", 0, 5), w("rf", 0, 5), 8.0, None, A.mult)
+    ts(w("rs", 1, 2), w("rf", 1, 2), 8.0, None, A.mult)
     ts(w("rs", 5, 6), w("rf", 2, 3), 32.0, None, A.mult)
+    ts(w("rs", 6, 7), w("rf", 2, 3), 4096.0, -7 * 4096.0, A.mult, A.add)
+    ts(w("rs", 2, 3), w("rf", 4, 5), 1000.0, k, A.mult, A.add)
+    ts(w("rs", 4, 5), w("rf", 4, 5), -1000.0, k, A.mult, A.add)
     sel(4, 8)
     ts(w("lst", L_A, L_A + 16), w("lf", L_A, L_A + 16), w("rs", 1, 2), w("rs", 5, 6), A.add, A.add)
     ts(w("lst", L_B, L_B + 16), w("lf", L_B, L_B + 16), w("rf", 0, 1), None, A.add)
     ts(w("idb"), w("n128"), k, None, A.is_equal)
     ts(w("idh"), w("n128"), k, None, A.is_equal)
-    act(w("idf"), w("idb"))
-    act(w("idn"), w("idb"), scale=-1.0)
+    ts(w("idn"), w("n128"), k, -1.0, A.is_equal, A.mult)
+    for n, c in enumerate((1.0, 8.0, 96.0, 56.0)):
+        act(idf(n), w("idb"), scale=c)
     sel(8, 16)
+    for to in range(2):
+        ts(mov(to, 0), w("n128"), w("rs", 2, 3), 16.0 * to, A.subtract, A.is_equal)
+        ts(mov(to, 1), w("n128"), w("rs", 4, 5), 16.0 * to + 984.0, A.subtract, A.is_equal)
+    ts(w("e8", rows=8), w("m16", rows=8), 0.0625, w("kc", 0, 1, rows=8), A.mult, A.is_equal)
+    fill(w("inj"), 0.0)
+    fill(w("dd", 256, 2 * PAD, PAD), 0.0)
+    ts(w("grp", 0, 8), w("n128", 0, 8), w("rf", 3, 4), -8.0, A.is_equal, A.mult)
+    ts(w("grp", 8, 16), w("n128", 0, 8), w("rf", 3, 4), 8.0, A.is_equal, A.mult)
 
     def weights(bank, chunk):
         h, c = chunk // 4, chunk % 4
@@ -249,45 +268,125 @@ def rank_program(g, core, T, topo):
             t = 2 * s + h
             mm(w(bank, s, 512, 8), w("sel", t * 128, t * 128 + 128), w("wtb", c * 64, c * 64 + 64))
 
+    def wt(c, a=0, b=512):
+        if c in RESIDENT:
+            return w(RESIDENT[c], a, b)
+        return w("wsb", IN_SBUF[c] * 512 + a, IN_SBUF[c] * 512 + b)
+
     cp(w("z0"), ind(w("sri"), w("lst", L_A, L_A + 16)))
     for b in range(2):
         cp(w("wtb", b, 256, 2), w("wti", b * 128, b * 128 + 128))
-    weights("px0", 0)
-    weights("px1", 1)
+    for c, bank in ((0, "px0"), (4, "px1"), (3, "pk0"), (5, "pk1")):
+        weights(bank, c)
+        act(wt(c), w(bank))
     turn(w("z1"), w("z0"))
-    ts(w("e8", rows=8), w("m16", rows=8), 0.0625, w("kc", 0, 1, rows=8), A.mult, A.is_equal)
     ts(w("zh"), ind(w("z1"), w("lst", L_B, L_B + 16)), -2048.0, None, A.add)
-    for g0 in range(2):
-        for g21 in range(4):
-            for h in range(2):
-                a = h * 128 + (g21 * 2 + g0) * 16
-                n = g21 * 32 + h * 16
-                mm(w("pk", a, a + 16), w("zh", g0 * 128, g0 * 128 + 128), w("idh", n, n + 16))
-    cp(w("bsh", rows=8), w("bsi", rows=8))
-    weights("pw2", 6)
-    ts(w("src"), w("pk", 0, 256), 2048.0, None, A.add)
     for h in range(2):
-        mm(w("pk", h * 128, h * 128 + 128), w("src", h * 128, h * 128 + 128), w("idf"))
-    weights("pw3", 7)
-    weights("pw0", 2)
-    weights("pw1", 3)
-    act(w("wsb", 0, 512), w("px0"))
-    act(w("wsb", 512, 1024), w("px1"))
-    act(w("wsb", 1024, 1536), w("pw2"))
-    act(w("wsb", 1536, 2048), w("pw3"))
-    weights("pw2", 4)
-    weights("pw3", 5)
-    fill(w("d2"), 1.0)
-    ts(w("grp", 0, 8), w("n128", 0, 8), w("rf", 3, 4), -8.0, A.is_equal, A.mult)
-    ts(w("grp", 8, 16), w("n128", 0, 8), w("rf", 3, 4), 8.0, A.is_equal, A.mult)
-    ts(w("rs", 6, 7), k, 128.0, None, A.add)
-    fill(w("d2", 0, 512, 8), 0.0)
-    cp(w("off"), w("pk", 0, 256))
-    ts(w("lst", L_F, L_F + 16), w("lf", L_F, L_F + 16), w("rf", 0, 1), None, A.add)
-    ts(w("lst", L_BC, L_BC + 8), w("lf", L_BC, L_BC + 8), w("rf", 1, 2), None, A.add)
-    ts(w("lst", L_T, L_T + 4), w("lf", L_T, L_T + 4), w("rs", 0, 1), None, A.add)
-    ts(w("lst", L_K, L_K + 2), w("lf", L_S, L_S + 2), w("rs", 4, 5), None, A.add)
+        for g0 in range(2):
+            mm(w(lu[h], 0, 128), mov(g0, h), w("zh", g0 * 128, g0 * 128 + 128), g0 == 0, g0 == 1)
+        mm(w(lu[h], 128, 256), w("one", rows=1), w("seed", rows=1), True, False)
+        for g0 in range(2):
+            mm(w(lu[h], 128, 256), w("zh", g0 * 128, g0 * 128 + 128), mov(g0, h), False, g0 == 1)
+    for h in range(2):
+        for b in range(2):
+            cp(w("bsh", h * 256 + b, h * 256 + 256, 2, rows=8),
+               w("bsi", h * 256 + b * 128, h * 256 + b * 128 + 128, rows=8))
+    for c in RESIDENT:
+        weights(RESIDENT[c], c)
+    for h in range(2):
+        ts(w("off", h * 128, h * 128 + 128), w(lu[h], 0, 128), 2048.0, None, A.add)
+    for c, bank in ((6, "px0"), (7, "px1")):
+        weights(bank, c)
+        cp(wt(c), w(bank))
+    for h in range(2):
+        act(w("src", h * 128, h * 128 + 128), w(lu[h], 128, 256))
 
+    later = []
+
+    def steps(r, h):
+        last = r == RO - 1
+        a = h * 256
+        d = h * PAD
+        src = w("src", h * 128, h * 128 + 128)
+
+        def largest():
+            scan(w("mx", a, a + 256), w("d1"), w(pk[h], 0, 256), A.add, A.max)
+
+        def records():
+            tt(w("nq", a, a + 256), w(pk[h], 0, 256), w("mx", a, a + 256), A.not_equal)
+
+        def carry(kind):
+            c = a + kind * 128
+            scan(w("sc", c, c + 128), w("nq", c, c + 128), src, A.mult, A.max)
+
+        def worst():
+            carry(0)
+
+        def best():
+            carry(1)
+            mm(w(px[h], 0, 32), idf(1), w("sc", a + 7, a + 256, 8), True, False)
+            mm(w(px[h], 16, 30), idf(0), w("mx", a + 128 + 23, a + 256, 8), False, False)
+            mm(w(px[h], 30, 32), idf(0), w("mx", a + 128 + 7, a + 128 + 16, 8), False, False)
+            mm(w(px[h], 16, 32), idf(3), w("sc", a + 7, a + 128, 8), False, False)
+            mm(w(px[h], 16, 32), idf(2), w("sc", a + 128 + 7, a + 256, 8), False, True)
+            mm(w(lu[h], 0, 128), src, idf(0), True, False)
+
+        def whole():
+            cp(w("zi", h * 32, h * 32 + 32), w(px[h], 0, 32))
+
+        def modulo():
+            ts(w("nw", h * 32, h * 32 + 32), w("zi", h * 32, h * 32 + 32), 3, 4095,
+               A.arith_shift_right, A.bitwise_and)
+
+        def terms(which):
+            old, new = [], []
+            for blk, plus, minus in ((0, "idn", "idh"), (1, "idh", "idn")):
+                if which == 0:
+                    old.append((w("inj", a + blk * 128, a + blk * 128 + 128), plus))
+                else:
+                    new.append((w("dd", d + blk * 128 + 1, d + blk * 128 + 129), plus))
+                    new.append((w("dd", d + blk * 128, d + blk * 128 + 128), minus))
+            return old + new
+
+        def inject():
+            ts(w("inj", a + 7, a + 256, 8), w("nw", h * 32, h * 32 + 32), -2048.0, None, A.add)
+            for x, sign in terms(0):
+                mm(w(lu[h], 0, 128), x, w(sign), False, False)
+
+        def back(blk):
+            scan(w("dd", d + blk * 128, d + blk * 128 + 128, -1), w("inj", a + blk * 128, a + blk * 128 + 128, -1),
+                 w("nq", a, a + 128, -1), A.add, A.mult)
+
+        def back_old():
+            back(0)
+
+        def back_new():
+            back(1)
+            ts_ = terms(1)
+            for n, (x, sign) in enumerate(ts_):
+                mm(w(lu[h], 0, 128), x, w(sign), False, n == len(ts_) - 1)
+
+        def listed():
+            if last:
+                ts(w("zh", h * 128, h * 128 + 128), w(lu[h], 0, 128), w("rs", 6, 7), -2048.0, A.add, A.add)
+                if h == 0:
+                    mm(w("pw0", 0, 256), w("one", rows=1), w("mid", rows=1), True, False)
+                for x in range(8):
+                    for g0 in range(2):
+                        c = x * 32 + g0 * 16
+                        mm(w("pw0", c, c + 16), mov(h, g0), w("zh", h * 128 + x * 16, h * 128 + x * 16 + 16),
+                           False, h == 1 and x == 7 and g0 == 1)
+            else:
+                ts(w("off", h * 128, h * 128 + 128), w(lu[h], 0, 128), w("rs", 6, 7), None, A.add)
+                mm(w(lu[h], 128, 256), idf(0), src, True, False)
+                ts_ = terms(0) + terms(1)
+                for n, (x, sign) in enumerate(ts_):
+                    mm(w(lu[h], 128, 256), w(sign), x, False, n == len(ts_) - 1)
+                later.append(lambda: act(src, w(lu[h], 128, 256)))
+
+        return [largest, records, worst, best, whole, modulo, inject, back_old, back_new, listed]
+
+    left = []
     for r in range(RO):
         last = r == RO - 1
         tab = w("tab%d" % r)
@@ -298,140 +397,100 @@ def rank_program(g, core, T, topo):
                 return w("aout", h * 256 + a, h * 256 + b)
             return w("tab%d" % (r + 1), rank * 512 + h * 256 + a, rank * 512 + h * 256 + b)
 
-        def gather(c0, c1):
-            act(w("p", c0 * 512, c1 * 512), ind(tab, w("off", c0 * 32, c1 * 32)), ext=arrived)
+        def gather(c, a=0, b=512):
+            act(w("p", c * 512 + a, c * 512 + b), ind(tab, w("off", c * 32 + a // 16, c * 32 + b // 16)),
+                ext=arrived)
 
-        def gather_mul(c0, c1):
-            a = c0 * 512 if c0 < 4 else (c0 - 4) * 512
-            tt(w("wp", c0 * 512, c1 * 512), ind(tab, w("off", c0 * 32, c1 * 32)),
-               w("wsb", a, a + (c1 - c0) * 512), A.mult, ext=arrived)
+        def gather_mul(c, a=0, b=512):
+            tt(w("wp", c * 512 + a, c * 512 + b), ind(tab, w("off", c * 32 + a // 16, c * 32 + b // 16)),
+               wt(c, a, b), A.mult, ext=arrived)
 
-        def mul(c):
-            tt(w("wp", c * 512, c * 512 + 512), w("p", c * 512, c * 512 + 512), w("pw%d" % (c - 2)), A.mult)
+        def mul(c, a=0, b=512):
+            tt(w("wp", c * 512 + a, c * 512 + b), w("p", c * 512 + a, c * 512 + b), wt(c, a, b), A.mult)
 
-        def bias(h):
+        def begin(h):
             mm(w(px[h], 0, 256), w("e8", rows=8), w("bsh", h * 256, h * 256 + 256, rows=8), True, False)
+            mm(w(pk[h], 0, 256), w("one", rows=1), w("tie", rows=1), True, False)
 
-        def wires(qt, stop):
-            h, mh = qt // 2, qt % 2
-            for b in range(2):
-                for s in range(8):
-                    a = b * 128 + mh * 64
-                    mm(w(px[h], a, a + 64), w("idh"), w("wp", qt * 1024 + b * 8 + s, qt * 1024 + 1024, 16),
-                       False, stop and b == 1 and s == 7)
+        def wires(c, stop=False):
+            a = c % 4 * 64
+            for s in range(8):
+                mm(w(px[c // 4], a, a + 64), w("idh"), w("wp", c * 512 + s, c * 512 + 512, 8), False, stop and s == 7)
 
         def clamp(h):
-            if h in clamp_s:
-                act(w("neg", h * 256, h * 256 + 256), w(px[h], 0, 256), -1.0, f=RELU, bias=255.0)
-                act(new_a(h), w("neg", h * 256, h * 256 + 256), -1.0, f=RELU, bias=255.0)
-            else:
-                ts(new_a(h), w(px[h], 0, 256), 0.0, 255.0, A.max, A.min)
+            for b in range(2):
+                ts(new_a(h, b * 128, b * 128 + 128), w(px[h], b, 256, 2), 0.0, 255.0, A.max, A.min)
             if last:
                 store("y", T.ya[:, h * 256:h * 256 + 256], new_a(h), "oy%d" % h)
             else:
                 send(r + 1, new_a(h), h)
-
-        def spread(h):
             for b in range(2):
                 mm(w(px[h], 256 + b, 512, 2), w("idb"), new_a(h, b * 128, b * 128 + 128))
 
-        def score_mul(h, s):
+        def score(h, s):
             a = (h * 8 + s) * 256
             tt(w("q", a, a + 256), w("p", h * 2048 + s, h * 2048 + 2048, 8), w(px[h], 256, 512), A.mult)
-
-        def score_sum(h, s):
-            a = (h * 8 + s) * 256
             for b in range(2):
-                mm(w("pk", h * 256 + b * 8 + s, h * 256 + 256, 16), w("q", a + b, a + 256, 2), w("grp"),
-                   False, h == 1 and s == 7 and b == 1)
+                mm(w(pk[h], b * 8 + s, 256, 16), w("q", a + b, a + 256, 2), w("grp"), False, s == 7 and b == 1)
 
-        def score(h, s):
-            score_mul(h, s)
-            score_sum(h, s)
+        def take(lst, n):
+            for _ in range(min(n, len(lst))):
+                lst.pop(0)()
 
-        def renew(h):
-            tt(w("src", h * 128, h * 128 + 128), w("ps", h * 256, h * 256 + 128),
-               w("nu", h * 128, h * 128 + 128), A.subtract)
-
-        bias(0)
-        bias(1)
-        mm(w("pk"), w("one", rows=1), w("tie", rows=1), True, False)
-        gather(2, 3)
-        gather_mul(0, 2)
-        gather(3, 4)
-        wires(0, False)
-        gather(4, 5)
+        begin(0)
+        gather(1)
+        gather(2)
+        gather(3)
+        gather_mul(0, 0, 256)
+        take(left, 1)
+        gather_mul(0, 256, 512)
+        wires(0)
+        take(left, 1)
+        mul(1, 0, 256)
+        take(left, 1)
+        mul(1, 256, 512)
+        wires(1)
+        take(left, 2)
         mul(2)
+        wires(2)
+        take(left, 1)
+        begin(1)
+        gather(5)
+        gather_mul(4)
+        wires(4)
         mul(3)
-        gather(5, 6)
-        wires(1, True)
-        gather_mul(6, 7)
-        if 0 not in clamp_s:
-            gather(0, 2)
-        clamp(0)
-        if 0 in clamp_s:
-            gather(0, 2)
-        spread(0)
-        gather_mul(7, 8)
-        wires(3, False)
-        mul(4)
+        wires(3, True)
+        gather(6)
         mul(5)
-        wires(2, True)
-        gather(6, 7)
-        score(0, 0)
-        score(0, 1)
+        wires(5)
+        clamp(0)
+        gather(7, 0, 256)
+        gather(7, 256, 512)
+        mul(6)
+        wires(6)
+        gather(0)
+        mul(7, 0, 256)
+        mul(7, 256, 512)
+        wires(7, True)
+        gather(4)
+        take(later, 2)
         clamp(1)
-        gather(7, 8)
         if not last:
             forward(r + 1)
-        for s in range(2, 8):
+        for s in range(8):
             score(0, s)
-            if s == 5:
-                spread(1)
-        for s in range(8):
+        first, second = steps(r, 0), steps(r, 1)
+        for s, n in enumerate((1, 1, 2, 0, 1, 1, 1, 2)):
             score(1, s)
-        if r:
-            renew(1)
-        else:
-            for h in range(2):
-                ts(w("em", h * 256, h * 256 + 256), w("en"), w("rs", 6, 7) if h else k, -1.0, A.is_equal, A.mult)
-        for h in range(2):
-            act(w("ps", h * 256, h * 256 + 128), w("src", h * 128, h * 128 + 128))
-            act(w("ps", h * 256 + 128, h * 256 + 256), w("src", h * 128, h * 128 + 128), scale=104.0)
-        if not last:
-            for h in range(2):
-                mm(w(px[h], 0, 128), w("src", h * 128, h * 128 + 128), w("idf"), True, False)
-
-        scan(w("mx"), w("d1"), w("pk"), A.add, A.max)
-        for s in range(8):
-            tt(w("oh", s, 512, 8), w("pk", s, 512, 8), w("mx", 7, 512, 8), A.is_equal)
-        act(w("kn"), ind(w("mx"), w("lst", L_K, L_K + 2)))
-        if last:
-            act(w("z0"), ind(w("src"), w("lst", L_F, L_F + 16)), f=IDENT, bias=-2048.0)
-        tt(w("pay"), w("oh"), w("ps"), A.mult)
-        scan(w("sc"), w("d2"), w("pay"), A.mult, A.add)
-        tt(w("za"), ind(w("sc"), w("lst", L_S, L_S + 2)), w("kn"), A.add)
-        act(w("zb"), ind(w("sc"), w("lst", L_T, L_T + 2)), scale=56.0)
-        tt(w("zi"), w("za"), w("zb"), A.add)
-        ts(w("nw"), w("zi"), 3, 4095, A.arith_shift_right, A.bitwise_and)
-        tt(w("nd"), ind(w("sc"), w("lst", L_T, L_T + 2)), w("nw"), A.subtract)
-        for h in range(2):
-            tt(w("nu", h * 128, h * 128 + 128), ind(w("nd", h * 16, h * 16 + 16), w("lst", L_BC, L_BC + 8)),
-               w("oh", h * 256, h * 256 + 128), A.mult)
-            if not last:
-                mm(w(px[h], 0, 128), w("nu", h * 128, h * 128 + 128), w("idn"), False, True)
-        if not last:
-            renew(0)
-            for h in range(2):
-                cp(w("off", h * 128, h * 128 + 128), w(px[h], 0, 128))
-        else:
-            tt(w("zh"), ind(w("nu"), w("lst", L_F, L_F + 16)), w("z0"), A.subtract)
-            for g0 in range(2):
-                mm(w("pk", 0, 256), w("zh", g0 * 128, g0 * 128 + 128), w("em", g0 * 256, g0 * 256 + 256),
-                   g0 == 0, g0 == 1)
-            turn(w("z2"), w("pk", 0, 256))
-            ts(w("z0"), ind(w("z2"), w("lst", L_A, L_A + 16)), 2048.0, None, A.add)
-            store("y", T.ys[:, :], w("z0"), "oys")
+            take(first, n)
+        take(second, 1)
+        take(first, 1)
+        take(second, 3)
+        left = second
+    take(left, len(left))
+    turn(w("z1"), w("pw0", 0, 256))
+    cp(w("z0"), ind(w("z1"), w("lst", L_A, L_A + 16)))
+    store("y", T.ys[:, :], w("z0"), "oys")
 
     def psum(name):
         return SCRATCH[name][0] == "psum"

@@ -3,17 +3,22 @@ from concourse.mybir import AluOpType, ActivationFunctionType
 
 RO = 3
 OPT = {
+    "clamp_s": (),
+    "fused": ((4, 5), (4, 5), (4, 5)),
+    "pieces": {7: ((0, 256), (256, 512))},
+    "hold_clamp": {"s": 150}, "hold_steps": {}, "wake": 200,
+    "land": 5.5, "start": 6.0,
     "forward": ((True, True), (True, True), (True, True)),
 }
-PAD = 272
-RESIDENT = {1: "pw0", 2: "pw1"}
-IN_SBUF = {0: 0, 4: 1, 3: 2, 5: 3, 6: 4, 7: 5}
+PAD = 136
+RESIDENT = {3: "pw0", 7: "pw1"}
+IN_SBUF = {0: 0, 1: 1, 2: 2, 4: 3, 5: 4, 6: 5}
 
 SCRATCH = {
     "tab0": ("sbuf", [128, 4096], "bfloat16"), "tab1": ("sbuf", [128, 4096], "bfloat16"),
     "tab2": ("sbuf", [128, 4096], "bfloat16"), "aout": ("sbuf", [128, 512], "bfloat16"),
     "p": ("sbuf", [128, 4096], "bfloat16"), "wp": ("sbuf", [128, 4096], "float16"),
-    "q": ("sbuf", [128, 4096], "float32"), "wsb": ("sbuf", [128, 3584], "bfloat16"),
+    "q": ("sbuf", [128, 4096], "float32"), "wsb": ("sbuf", [128, 3072], "bfloat16"),
     "off": ("sbuf", [128, 256], "uint16"),
     "sri": ("sbuf", [128, 256], "int32"), "wti": ("sbuf", [128, 256], "int32"), "bsi": ("sbuf", [128, 512], "int32"),
     "wtb": ("sbuf", [128, 256], "bfloat16"), "bsh": ("sbuf", [128, 512], "float16"),
@@ -21,22 +26,23 @@ SCRATCH = {
     "m16": ("sbuf", [128, 128], "bfloat16"), "lf": ("sbuf", [128, 32], "float32"),
     "zh": ("sbuf", [128, 256], "float16"), "neg": ("sbuf", [128, 512], "bfloat16"),
     "ki": ("sbuf", [128, 16], "int32"), "kj": ("sbuf", [128, 8], "int32"),
-    "rf": ("sbuf", [128, 8], "float32"), "rs": ("sbuf", [128, 8], "float32"),
+    "rf": ("sbuf", [128, 8], "float32"), "rs": ("sbuf", [128, 16], "float32"),
     "lst": ("sbuf", [128, 32], "uint16"),
     "sel": ("sbuf", [128, 2048], "bfloat16"), "mov": ("sbuf", [128, 512], "float16"),
-    "idf": ("sbuf", [128, 512], "float32"),
+    "fin": ("sbuf", [128, 512], "float16"), "idf": ("sbuf", [128, 512], "float32"),
     "idb": ("sbuf", [128, 128], "bfloat16"), "idh": ("sbuf", [128, 128], "float16"),
     "idn": ("sbuf", [128, 128], "float16"),
     "e8": ("sbuf", [128, 128], "float16"), "grp": ("sbuf", [128, 16], "float32"),
     "one": ("sbuf", [128, 128], "bfloat16"), "tie": ("sbuf", [128, 256], "bfloat16"),
-    "src": ("sbuf", [128, 256], "float32"), "seed": ("sbuf", [128, 128], "bfloat16"), "mid": ("sbuf", [128, 256], "bfloat16"),
+    "src": ("sbuf", [128, 256], "float32"), "seed": ("sbuf", [128, 128], "bfloat16"),
+    "mid": ("sbuf", [128, 256], "bfloat16"), "kn": ("sbuf", [128, 64], "float32"),
     "d1": ("sbuf", [128, 256], "bfloat16"),
     "z0": ("sbuf", [128, 256], "float32"), "z1": ("sbuf", [128, 256], "float32"),
     "mx": ("sbuf", [128, 512], "float32"), "nq": ("sbuf", [128, 512], "float16"),
     "sc": ("sbuf", [128, 512], "float32"),
     "zi": ("sbuf", [128, 64], "int32"), "nw": ("sbuf", [128, 64], "int32"),
-    "inj": ("sbuf", [128, 512], "float16"), "dd": ("sbuf", [128, 2 * PAD], "float16"),
-    "pw0": ("psum", [128, 512], "float32"), "pw1": ("psum", [128, 512], "float32"),
+    "inj": ("sbuf", [128, 512], "float16"), "dd": ("sbuf", [128, 4 * PAD], "float16"),
+    "pw0": ("psum", [128, 16, 32], "float32"), "pw1": ("psum", [128, 16, 32], "float32"),
     "px0": ("psum", [128, 512], "float32"), "px1": ("psum", [128, 512], "float32"),
     "pk0": ("psum", [128, 512], "float32"), "pk1": ("psum", [128, 512], "float32"),
     "lu0": ("psum", [128, 512], "float32"), "lu1": ("psum", [128, 512], "float32"),
@@ -57,6 +63,7 @@ def rank_program(g, core, T, topo):
     queue = {"v": g.vector, "s": g.scalar, "t": g.tensor, "g": g, "y": g.sync}
     own_sem = {"v": "cv", "s": "cs", "t": "ct", "g": "cg"}
     ops = []
+    hold = [{}]
     fwd = OPT["forward"]
 
     def w(name, a=0, b=None, st=1, rows=128):
@@ -75,6 +82,13 @@ def rank_program(g, core, T, topo):
             ap = T[name][0:rows, a:b:st]
         return (name, ap, bits)
 
+    def w3(name, a, b, c=0, d=32, st=1):
+        bits = 0
+        for x in range(a, b):
+            for y in range(c, d, st):
+                bits |= 1 << (x * 32 + y)
+        return (name, T[name][:, a, c:d:st] if b == a + 1 else T[name][:, a:b, c:d:st], bits)
+
     def ind(win, lst):
         return ("", win[1].indirect(lst[1]), 0, [win, lst])
 
@@ -86,14 +100,41 @@ def rank_program(g, core, T, topo):
     def val(x):
         return x[1] if isinstance(x, tuple) else x
 
-    def op(q, fn, reads, writes, ext=(), dma=None, mute=False):
+    def psum(name):
+        return SCRATCH[name][0] == "psum"
+
+    def count(x):
+        return bin(x[2]).count("1")
+
+    def wide(x):
+        return SCRATCH[x[0]][2] in ("float32", "int32")
+
+    def cycles(q, reads, writes, both):
+        full = [x for x in reads if isinstance(x, tuple) and len(x) == 3 and count(x) > 1]
+        if q == "t":
+            return max(min(64, count(reads[0])), count(reads[1])) * (4 if wide(reads[0]) else 1) / 2
+        if q == "g" and writes:
+            return 160 + 2 * count(writes[0])
+        if q not in "vs" or not writes:
+            return 300
+        n = count(writes[0])
+        if any(isinstance(x, tuple) and len(x) == 4 for x in reads):
+            return 70 + 1.56 * n
+        if q == "v" and both and not any(psum(x[0]) for x in full):
+            n *= 2
+        if q == "v" and not any(wide(x) for x in full + writes):
+            n /= 2
+        return 12 + max(64, n)
+
+    def op(q, fn, reads, writes, ext=(), dma=None, mute=False, both=False):
         rd = []
         for x in reads:
             rd += parts(x)
-        ops.append({"q": q, "fn": fn, "r": rd, "w": list(writes), "ext": list(ext), "dma": dma, "mute": mute})
+        ops.append({"q": q, "fn": fn, "r": rd, "w": list(writes), "ext": list(ext), "dma": dma, "mute": mute,
+                    "hold": hold[0].get(q, 0), "cost": 80 if dma else cycles(q, reads, list(writes), both)})
 
     def tt(out, a, b, f, ext=()):
-        op("v", lambda: g.vector.tensor_tensor(out[1], a[1], b[1], f), [a, b], [out], ext)
+        op("v", lambda: g.vector.tensor_tensor(out[1], a[1], b[1], f), [a, b], [out], ext, both=True)
 
     def ts(out, a, s1, s2, f0, f1=None):
         if f1 is None:
@@ -171,6 +212,7 @@ def rank_program(g, core, T, topo):
                                         remote_sem=T.sem["near%d" % r], srcs=[b[1]], dsts=[b[1]]))
             sent[0] += len(e_near)
         op("g", lambda: g.remote_dma_fused(tr, local_sem=T.sem.sent), [b], [], mute=True)
+        ops[-1]["sends"] = r
 
     def forward_call(r, h, call):
         tr = []
@@ -210,73 +252,64 @@ def rank_program(g, core, T, topo):
     send(0, w("tab0", rank * 512, rank * 512 + 512), 0, to_far=False)
     forward(0)
 
-    fill(w("one", rows=32), 1.0)
-    fill(w("d1"), 0.0)
-    for s in range(8):
-        act(w("tie", s, 256, 8, rows=1), w("one", 0, 32, rows=1), scale=float(7 - s))
-    act(w("seed", rows=1), w("tie", 0, 128, rows=1), scale=4096.0, f=IDENT, bias=2048.0)
-    act(w("mid", rows=1), w("tie", rows=1), scale=0.0, f=IDENT, bias=2048.0)
     k = w("kc", 0, 1)
     cp(w("ki"), w("kc"))
+    FIELDS = ((0, 15), (3, 1), (0, 7), (4, 7), (4, 1), (5, 3))
+    for n, (shift, bits) in enumerate(FIELDS):
+        ts(w("kj", n, n + 1), w("ki", 0, 1), shift, bits, A.arith_shift_right, A.bitwise_and)
+    cp(w("rf", 0, len(FIELDS)), w("kj", 0, len(FIELDS)))
+    low4, bit3, low3, group, bit4, top2 = [w("rf", n, n + 1) for n in range(len(FIELDS))]
 
-    def sel(t0, t1):
-        for t in range(t0, t1):
-            ts(w("sel", t * 128, t * 128 + 128), w("m16"), w("kc", t, t + 1), None, A.is_equal)
+    def col(n):
+        return w("rs", n, n + 1)
+
+    ts(col(0), bit3, 8.0, None, A.mult)
+    ts(col(1), low3, 32.0, None, A.mult)
+    ts(w("lst", L_A, L_A + 16), w("lf", L_A, L_A + 16), col(0), col(1), A.add, A.add)
+    ts(w("lst", L_B, L_B + 16), w("lf", L_B, L_B + 16), low4, None, A.add)
+    for t in range(16):
+        ts(w("sel", t * 128, t * 128 + 128), w("m16"), w("kc", t, t + 1), None, A.is_equal)
 
     def mov(to, frm):
         a = (to * 2 + frm) * 128
         return w("mov", a, a + 128)
 
+    def fin(to, frm):
+        a = (to * 2 + frm) * 128
+        return w("fin", a, a + 128)
+
     def idf(n):
         return w("idf", n * 128, n * 128 + 128)
 
-    fill(w("d1", 0, 256, 8), -3.0e7)
-    ts(w("kj", 0, 1), w("ki", 0, 1), 15, None, A.bitwise_and)
-    ts(w("kj", 1, 2), w("ki", 0, 1), 3, 1, A.arith_shift_right, A.bitwise_and)
-    ts(w("kj", 2, 3), w("ki", 0, 1), 7, None, A.bitwise_and)
-    ts(w("kj", 3, 4), w("ki", 0, 1), 4, None, A.arith_shift_right)
-    ts(w("kj", 4, 5), w("ki", 0, 1), 4, 1, A.arith_shift_right, A.bitwise_and)
-    sel(0, 2)
-    cp(w("rf", 0, 5), w("kj", 0, 5))
-    sel(2, 4)
-    ts(w("rs", 1, 2), w("rf", 1, 2), 8.0, None, A.mult)
-    ts(w("rs", 5, 6), w("rf", 2, 3), 32.0, None, A.mult)
-    ts(w("rs", 6, 7), w("rf", 2, 3), 4096.0, -7 * 4096.0, A.mult, A.add)
-    ts(w("rs", 2, 3), w("rf", 4, 5), 1000.0, k, A.mult, A.add)
-    ts(w("rs", 4, 5), w("rf", 4, 5), -1000.0, k, A.mult, A.add)
-    sel(4, 8)
-    ts(w("lst", L_A, L_A + 16), w("lf", L_A, L_A + 16), w("rs", 1, 2), w("rs", 5, 6), A.add, A.add)
-    ts(w("lst", L_B, L_B + 16), w("lf", L_B, L_B + 16), w("rf", 0, 1), None, A.add)
+    ts(col(2), bit4, 1000.0, k, A.mult, A.add)
+    ts(col(3), bit4, -1000.0, k, A.mult, A.add)
+    for to in range(2):
+        ts(mov(to, 0), w("n128"), col(2), 16.0 * to, A.subtract, A.is_equal)
+        ts(mov(to, 1), w("n128"), col(3), 16.0 * to + 984.0, A.subtract, A.is_equal)
+    fill(w("one", rows=32), 1.0)
+    for s in range(8):
+        act(w("tie", s, 256, 8, rows=1), w("one", 0, 32, rows=1), scale=float(7 - s))
+    act(w("seed", rows=1), w("tie", 0, 128, rows=1), scale=4096.0, f=IDENT, bias=2048.0)
     ts(w("idb"), w("n128"), k, None, A.is_equal)
     ts(w("idh"), w("n128"), k, None, A.is_equal)
-    ts(w("idn"), w("n128"), k, -1.0, A.is_equal, A.mult)
-    for n, c in enumerate((1.0, 8.0, 96.0, 56.0)):
-        act(idf(n), w("idb"), scale=c)
-    sel(8, 16)
-    for to in range(2):
-        ts(mov(to, 0), w("n128"), w("rs", 2, 3), 16.0 * to, A.subtract, A.is_equal)
-        ts(mov(to, 1), w("n128"), w("rs", 4, 5), 16.0 * to + 984.0, A.subtract, A.is_equal)
     ts(w("e8", rows=8), w("m16", rows=8), 0.0625, w("kc", 0, 1, rows=8), A.mult, A.is_equal)
-    fill(w("inj"), 0.0)
-    fill(w("dd", 256, 2 * PAD, PAD), 0.0)
-    ts(w("grp", 0, 8), w("n128", 0, 8), w("rf", 3, 4), -8.0, A.is_equal, A.mult)
-    ts(w("grp", 8, 16), w("n128", 0, 8), w("rf", 3, 4), 8.0, A.is_equal, A.mult)
 
     def weights(bank, chunk):
         h, c = chunk // 4, chunk % 4
         for s in range(8):
             t = 2 * s + h
-            mm(w(bank, s, 512, 8), w("sel", t * 128, t * 128 + 128), w("wtb", c * 64, c * 64 + 64))
+            mm(w3(bank, 0, 16, s, 32, 8) if chunk in RESIDENT else w(bank, s, 512, 8),
+               w("sel", t * 128, t * 128 + 128), w("wtb", c * 64, c * 64 + 64))
 
     def wt(c, a=0, b=512):
         if c in RESIDENT:
-            return w(RESIDENT[c], a, b)
+            return w3(RESIDENT[c], a // 32, b // 32)
         return w("wsb", IN_SBUF[c] * 512 + a, IN_SBUF[c] * 512 + b)
 
     cp(w("z0"), ind(w("sri"), w("lst", L_A, L_A + 16)))
     for b in range(2):
         cp(w("wtb", b, 256, 2), w("wti", b * 128, b * 128 + 128))
-    for c, bank in ((0, "px0"), (4, "px1"), (3, "pk0"), (5, "pk1")):
+    for c, bank in ((4, "px0"), (0, "px1"), (5, "pk0"), (1, "pk1")):
         weights(bank, c)
         act(wt(c), w(bank))
     turn(w("z1"), w("z0"))
@@ -284,109 +317,95 @@ def rank_program(g, core, T, topo):
     for h in range(2):
         for g0 in range(2):
             mm(w(lu[h], 0, 128), mov(g0, h), w("zh", g0 * 128, g0 * 128 + 128), g0 == 0, g0 == 1)
-        mm(w(lu[h], 128, 256), w("one", rows=1), w("seed", rows=1), True, False)
-        for g0 in range(2):
-            mm(w(lu[h], 128, 256), w("zh", g0 * 128, g0 * 128 + 128), mov(g0, h), False, g0 == 1)
+        ts(w("off", h * 128, h * 128 + 128), w(lu[h], 0, 128), 2048.0, None, A.add)
     for h in range(2):
         for b in range(2):
             cp(w("bsh", h * 256 + b, h * 256 + 256, 2, rows=8),
                w("bsi", h * 256 + b * 128, h * 256 + b * 128 + 128, rows=8))
+    for c, bank in ((2, "px0"), (6, "px1")):
+        weights(bank, c)
+        cp(wt(c), w(bank))
     for c in RESIDENT:
         weights(RESIDENT[c], c)
     for h in range(2):
-        ts(w("off", h * 128, h * 128 + 128), w(lu[h], 0, 128), 2048.0, None, A.add)
-    for c, bank in ((6, "px0"), (7, "px1")):
-        weights(bank, c)
-        cp(wt(c), w(bank))
-    for h in range(2):
-        act(w("src", h * 128, h * 128 + 128), w(lu[h], 128, 256))
+        mm(w(lu[h], 128, 256), w("one", rows=1), w("seed", rows=1), True, False)
+        for g0 in range(2):
+            mm(w(lu[h], 128, 256), w("zh", g0 * 128, g0 * 128 + 128), mov(g0, h), False, g0 == 1)
 
-    later = []
+    def late_constants():
+        ts(w("grp", 0, 8), w("n128", 0, 8), group, -8.0, A.is_equal, A.mult)
+        ts(w("grp", 8, 16), w("n128", 0, 8), group, 8.0, A.is_equal, A.mult)
+        fill(w("d1"), 0.0)
+        fill(w("d1", 0, 256, 8), -3.0e7)
+        fill(w("kn"), 0.0)
+        fill(w("inj"), 0.0)
+        fill(w("dd", 128, 4 * PAD, PAD), 0.0)
+        ts(w("idn"), w("n128"), k, -1.0, A.is_equal, A.mult)
+        ts(col(4), low3, 4096.0, -7 * 4096.0, A.mult, A.add)
+        for n, c in enumerate((1.0, 8.0, 104.0, 56.0)):
+            act(idf(n), w("idb"), scale=c)
+        act(w("mid", rows=1), w("tie", rows=1), scale=0.0, f=IDENT, bias=2048.0)
+        ts(col(5), top2, 32.0, bit3, A.mult, A.add)
+        ts(col(6), low3, 4.0, col(5), A.mult, A.add)
+        ts(col(7), bit4, 1000.0, col(6), A.mult, A.add)
+        ts(col(8), bit4, -1000.0, col(6), A.mult, A.add)
+        for to in range(2):
+            ts(fin(to, 0), w("n128"), col(7), 2.0 * to, A.subtract, A.is_equal)
+            ts(fin(to, 1), w("n128"), col(8), 2.0 * to + 1000.0, A.subtract, A.is_equal)
 
-    def steps(r, h):
-        last = r == RO - 1
-        a = h * 256
-        d = h * PAD
+    signs = (("idn", "idh"), ("idh", "idn"))
+
+    def put(h, blk):
+        a = h * 256 + blk * 128
+        return [(w("inj", a, a + 128), signs[blk][0])]
+
+    def carried(h, blk):
+        c = (2 * h + blk) * PAD
+        return [(w("dd", c + 1, c + 129), signs[blk][0]), (w("dd", c, c + 128), signs[blk][1])]
+
+    def sources(r, h):
         src = w("src", h * 128, h * 128 + 128)
+        if r:
+            mm(w(lu[h], 128, 256), idf(0), src, True, False)
+            terms = put(h, 0) + put(h, 1) + carried(h, 0) + carried(h, 1)
+            for n, (x, sign) in enumerate(terms):
+                mm(w(lu[h], 128, 256), w(sign), x, False, n == len(terms) - 1)
+        act(src, w(lu[h], 128, 256))
+        mm(w(lu[h], 0, 128), src, idf(0), True, False)
 
-        def largest():
-            scan(w("mx", a, a + 256), w("d1"), w(pk[h], 0, 256), A.add, A.max)
-
-        def records():
-            tt(w("nq", a, a + 256), w(pk[h], 0, 256), w("mx", a, a + 256), A.not_equal)
-
-        def carry(kind):
-            c = a + kind * 128
-            scan(w("sc", c, c + 128), w("nq", c, c + 128), src, A.mult, A.max)
-
-        def worst():
-            carry(0)
-
-        def best():
-            carry(1)
-            mm(w(px[h], 0, 32), idf(1), w("sc", a + 7, a + 256, 8), True, False)
-            mm(w(px[h], 16, 30), idf(0), w("mx", a + 128 + 23, a + 256, 8), False, False)
-            mm(w(px[h], 30, 32), idf(0), w("mx", a + 128 + 7, a + 128 + 16, 8), False, False)
-            mm(w(px[h], 16, 32), idf(3), w("sc", a + 7, a + 128, 8), False, False)
-            mm(w(px[h], 16, 32), idf(2), w("sc", a + 128 + 7, a + 256, 8), False, True)
-            mm(w(lu[h], 0, 128), src, idf(0), True, False)
-
-        def whole():
-            cp(w("zi", h * 32, h * 32 + 32), w(px[h], 0, 32))
-
-        def modulo():
-            ts(w("nw", h * 32, h * 32 + 32), w("zi", h * 32, h * 32 + 32), 3, 4095,
-               A.arith_shift_right, A.bitwise_and)
-
-        def terms(which):
-            old, new = [], []
-            for blk, plus, minus in ((0, "idn", "idh"), (1, "idh", "idn")):
-                if which == 0:
-                    old.append((w("inj", a + blk * 128, a + blk * 128 + 128), plus))
-                else:
-                    new.append((w("dd", d + blk * 128 + 1, d + blk * 128 + 129), plus))
-                    new.append((w("dd", d + blk * 128, d + blk * 128 + 128), minus))
-            return old + new
-
-        def inject():
-            ts(w("inj", a + 7, a + 256, 8), w("nw", h * 32, h * 32 + 32), -2048.0, None, A.add)
-            for x, sign in terms(0):
-                mm(w(lu[h], 0, 128), x, w(sign), False, False)
-
-        def back(blk):
-            scan(w("dd", d + blk * 128, d + blk * 128 + 128, -1), w("inj", a + blk * 128, a + blk * 128 + 128, -1),
+    def choose(r, h):
+        a, n = h * 256, h * 32
+        src = w("src", h * 128, h * 128 + 128)
+        scan(w("mx", a, a + 256), w("d1"), w(pk[h], 0, 256), A.add, A.max)
+        act(w("kn", n + 16, n + 30), w("mx", a + 128 + 23, a + 256, 8))
+        act(w("kn", n + 30, n + 32), w("mx", a + 128 + 7, a + 128 + 16, 8))
+        tt(w("nq", a, a + 256), w(pk[h], 0, 256), w("mx", a, a + 256), A.not_equal)
+        scan(w("sc", a, a + 128), w("nq", a, a + 128), src, A.mult, A.max)
+        mm(w(px[h], 0, 16), idf(1), w("sc", a + 7, a + 128, 8))
+        mm(w(px[h], 16, 32), idf(3), w("sc", a + 7, a + 128, 8), True, False)
+        scan(w("sc", a + 128, a + 256), w("nq", a + 128, a + 256), src, A.mult, A.max)
+        mm(w(px[h], 16, 32), idf(2), w("sc", a + 128 + 7, a + 256, 8), False, True)
+        tt(w("zi", n, n + 32), w(px[h], 0, 32), w("kn", n, n + 32), A.add)
+        ts(w("nw", n, n + 32), w("zi", n, n + 32), 3, 4095, A.arith_shift_right, A.bitwise_and)
+        ts(w("inj", a + 7, a + 256, 8), w("nw", n, n + 32), -2048.0, None, A.add)
+        for x, sign in put(h, 0) + put(h, 1):
+            mm(w(lu[h], 0, 128), x, w(sign), False, False)
+        for blk in range(2):
+            c = (2 * h + blk) * PAD
+            scan(w("dd", c, c + 128, -1), w("inj", a + blk * 128, a + blk * 128 + 128, -1),
                  w("nq", a, a + 128, -1), A.add, A.mult)
+            for m, (x, sign) in enumerate(carried(h, blk)):
+                mm(w(lu[h], 0, 128), x, w(sign), False, blk == 1 and m == 1)
+        if r < RO - 1:
+            ts(w("off", h * 128, h * 128 + 128), w(lu[h], 0, 128), col(4), None, A.add)
+        else:
+            ts(w("zh", h * 128, h * 128 + 128), w(lu[h], 0, 128), col(4), -2048.0, A.add, A.add)
+            if h == 0:
+                mm(w3("pw0", 0, 8), w("one", rows=1), w("mid", rows=1), True, False)
+            for g0 in range(2):
+                mm(w3("pw0", 0, 8, g0 * 16, g0 * 16 + 16), fin(h, g0), w("zh", h * 128, h * 128 + 128),
+                   False, h == 1 and g0 == 1)
 
-        def back_old():
-            back(0)
-
-        def back_new():
-            back(1)
-            ts_ = terms(1)
-            for n, (x, sign) in enumerate(ts_):
-                mm(w(lu[h], 0, 128), x, w(sign), False, n == len(ts_) - 1)
-
-        def listed():
-            if last:
-                ts(w("zh", h * 128, h * 128 + 128), w(lu[h], 0, 128), w("rs", 6, 7), -2048.0, A.add, A.add)
-                if h == 0:
-                    mm(w("pw0", 0, 256), w("one", rows=1), w("mid", rows=1), True, False)
-                for x in range(8):
-                    for g0 in range(2):
-                        c = x * 32 + g0 * 16
-                        mm(w("pw0", c, c + 16), mov(h, g0), w("zh", h * 128 + x * 16, h * 128 + x * 16 + 16),
-                           False, h == 1 and x == 7 and g0 == 1)
-            else:
-                ts(w("off", h * 128, h * 128 + 128), w(lu[h], 0, 128), w("rs", 6, 7), None, A.add)
-                mm(w(lu[h], 128, 256), idf(0), src, True, False)
-                ts_ = terms(0) + terms(1)
-                for n, (x, sign) in enumerate(ts_):
-                    mm(w(lu[h], 128, 256), w(sign), x, False, n == len(ts_) - 1)
-                later.append(lambda: act(src, w(lu[h], 128, 256)))
-
-        return [largest, records, worst, best, whole, modulo, inject, back_old, back_new, listed]
-
-    left = []
     for r in range(RO):
         last = r == RO - 1
         tab = w("tab%d" % r)
@@ -397,29 +416,33 @@ def rank_program(g, core, T, topo):
                 return w("aout", h * 256 + a, h * 256 + b)
             return w("tab%d" % (r + 1), rank * 512 + h * 256 + a, rank * 512 + h * 256 + b)
 
-        def gather(c, a=0, b=512):
-            act(w("p", c * 512 + a, c * 512 + b), ind(tab, w("off", c * 32 + a // 16, c * 32 + b // 16)),
-                ext=arrived)
+        def picked(c, a, b):
+            return ind(tab, w("off", c * 32 + a // 16, c * 32 + b // 16))
 
-        def gather_mul(c, a=0, b=512):
-            tt(w("wp", c * 512 + a, c * 512 + b), ind(tab, w("off", c * 32 + a // 16, c * 32 + b // 16)),
-               wt(c, a, b), A.mult, ext=arrived)
+        def gather(c, a, b):
+            act(w("p", c * 512 + a, c * 512 + b), picked(c, a, b), ext=arrived)
 
-        def mul(c, a=0, b=512):
+        def gather_mul(c, a, b):
+            tt(w("wp", c * 512 + a, c * 512 + b), picked(c, a, b), wt(c, a, b), A.mult, ext=arrived)
+
+        def mul(c, a, b):
             tt(w("wp", c * 512 + a, c * 512 + b), w("p", c * 512 + a, c * 512 + b), wt(c, a, b), A.mult)
 
-        def begin(h):
-            mm(w(px[h], 0, 256), w("e8", rows=8), w("bsh", h * 256, h * 256 + 256, rows=8), True, False)
-            mm(w(pk[h], 0, 256), w("one", rows=1), w("tie", rows=1), True, False)
-
-        def wires(c, stop=False):
+        def wires(c):
             a = c % 4 * 64
             for s in range(8):
-                mm(w(px[c // 4], a, a + 64), w("idh"), w("wp", c * 512 + s, c * 512 + 512, 8), False, stop and s == 7)
+                mm(w(px[c // 4], a, a + 64), w("idh"), w("wp", c * 512 + s, c * 512 + 512, 8),
+                   False, c % 4 == 3 and s == 7)
 
         def clamp(h):
+            if h in OPT["clamp_s"]:
+                act(w("neg", h * 256, h * 256 + 256), w(px[h], 0, 256), -1.0, f=RELU, bias=255.0)
             for b in range(2):
-                ts(new_a(h, b * 128, b * 128 + 128), w(px[h], b, 256, 2), 0.0, 255.0, A.max, A.min)
+                if h in OPT["clamp_s"]:
+                    act(new_a(h, b * 128, b * 128 + 128), w("neg", h * 256 + b, h * 256 + 256, 2), -1.0,
+                        f=RELU, bias=255.0)
+                else:
+                    ts(new_a(h, b * 128, b * 128 + 128), w(px[h], b, 256, 2), 0.0, 255.0, A.max, A.min)
             if last:
                 store("y", T.ya[:, h * 256:h * 256 + 256], new_a(h), "oy%d" % h)
             else:
@@ -433,67 +456,85 @@ def rank_program(g, core, T, topo):
             for b in range(2):
                 mm(w(pk[h], b * 8 + s, 256, 16), w("q", a + b, a + 256, 2), w("grp"), False, s == 7 and b == 1)
 
-        def take(lst, n):
-            for _ in range(min(n, len(lst))):
-                lst.pop(0)()
-
-        begin(0)
-        gather(1)
-        gather(2)
-        gather(3)
-        gather_mul(0, 0, 256)
-        take(left, 1)
-        gather_mul(0, 256, 512)
-        wires(0)
-        take(left, 1)
-        mul(1, 0, 256)
-        take(left, 1)
-        mul(1, 256, 512)
-        wires(1)
-        take(left, 2)
-        mul(2)
-        wires(2)
-        take(left, 1)
-        begin(1)
-        gather(5)
-        gather_mul(4)
-        wires(4)
-        mul(3)
-        wires(3, True)
-        gather(6)
-        mul(5)
-        wires(5)
-        clamp(0)
-        gather(7, 0, 256)
-        gather(7, 256, 512)
-        mul(6)
-        wires(6)
-        gather(0)
-        mul(7, 0, 256)
-        mul(7, 256, 512)
-        wires(7, True)
-        gather(4)
-        take(later, 2)
-        clamp(1)
+        for h in range(2):
+            mm(w(px[h], 0, 256), w("e8", rows=8), w("bsh", h * 256, h * 256 + 256, rows=8), True, False)
+            for c in range(4 * h, 4 * h + 4):
+                for a, b in OPT["pieces"].get(c, ((0, 512),)):
+                    if c in OPT["fused"][r]:
+                        gather_mul(c, a, b)
+                    else:
+                        gather(c, a, b)
+                        mul(c, a, b)
+                wires(c)
+            hold[0] = OPT["hold_clamp"]
+            clamp(h)
+            hold[0] = {}
+        for c in OPT["fused"][r]:
+            gather(c, 0, 256)
+            gather(c, 256, 512)
         if not last:
             forward(r + 1)
-        for s in range(8):
-            score(0, s)
-        first, second = steps(r, 0), steps(r, 1)
-        for s, n in enumerate((1, 1, 2, 0, 1, 1, 1, 2)):
-            score(1, s)
-            take(first, n)
-        take(second, 1)
-        take(first, 1)
-        take(second, 3)
-        left = second
-    take(left, len(left))
-    turn(w("z1"), w("pw0", 0, 256))
-    cp(w("z0"), ind(w("z1"), w("lst", L_A, L_A + 16)))
+        if r == 0:
+            late_constants()
+        for h in range(2):
+            mm(w(pk[h], 0, 256), w("one", rows=1), w("tie", rows=1), True, False)
+            for s in range(8):
+                score(h, s)
+            sources(r, h)
+            hold[0] = OPT["hold_steps"]
+            choose(r, h)
+            hold[0] = {}
+    for x in range(8):
+        turn(w("z0", x, 256, 8), w3("pw0", x, x + 1))
     store("y", T.ys[:, :], w("z0"), "oys")
 
-    def psum(name):
-        return SCRATCH[name][0] == "psum"
+    def arrange(ops):
+        WAKE, DMA = OPT["wake"], 2700
+        before = [dict() for _ in ops]
+        seen, last_send, last_of = {}, {}, {}
+        for n, o in enumerate(ops):
+            for views, writing in ((o["r"], False), (o["w"], True)):
+                for name, _, bits in views:
+                    for m, mbits, mw in seen.get(name, []):
+                        if (mw or writing) and (psum(name) or mbits & bits) and not ops[m]["mute"]:
+                            both_t = ops[m]["q"] == "t" and o["q"] == "t"
+                            before[n][m] = DMA if ops[m]["dma"] else 0 if both_t else WAKE
+            for views, writing in ((o["r"], False), (o["w"], True)):
+                for name, _, bits in views:
+                    seen.setdefault(name, []).append((n, bits, writing))
+            if o["q"] in "gy" or o["dma"]:
+                if o["q"] in last_of:
+                    before[n].setdefault(last_of[o["q"]], 0)
+                last_of[o["q"]] = n
+            if "sends" in o:
+                last_send[o["sends"]] = n
+            elif o["ext"] and o["q"] != "g":
+                r = int(o["ext"][0][0][3])
+                before[n][last_send[r]] = (OPT["land"] if r else OPT["start"]) / 0.83e-3
+        after = [[] for _ in ops]
+        for n, b in enumerate(before):
+            for m in b:
+                after[m].append(n)
+        waiting = [len(b) for b in before]
+        ready = {q: [n for n, o in enumerate(ops) if o["q"] == q and not waiting[n]] for q in queue}
+        can = [0.0] * len(ops)
+        free = {q: 0.0 for q in queue}
+        order = []
+        while len(order) < len(ops):
+            q = min((q for q in queue if ready[q]), key=lambda q: max(free[q], min(can[n] for n in ready[q])))
+            now = max(free[q], min(can[n] for n in ready[q]))
+            n = min(n for n in ready[q] if can[n] <= now + ops[n]["hold"])
+            ready[q].remove(n)
+            order.append(n)
+            free[q] = max(now, can[n]) + ops[n]["cost"]
+            for m in after[n]:
+                can[m] = max(can[m], free[q] + before[m][n])
+                waiting[m] -= 1
+                if not waiting[m]:
+                    ready[ops[m]["q"]].append(m)
+        return [ops[n] for n in order]
+
+    ops = arrange(ops)
 
     history = {}
     for n, o in enumerate(ops):
@@ -527,7 +568,7 @@ def rank_program(g, core, T, topo):
             ops[m]["signal"] = True
         o["need"] = sorted(need.values())
 
-    count = {q: 0 for q in queue}
+    done = {q: 0 for q in queue}
     waited = {q: set() for q in queue}
     for o in ops:
         q = o["q"]
@@ -542,9 +583,9 @@ def rank_program(g, core, T, topo):
             ins.then_inc(T.sem[o["dma"]], 16)
             o["token"] = (o["dma"], 16)
         elif o.get("signal"):
-            count[q] += 1
+            done[q] += 1
             ins.then_inc(T.sem[own_sem[q]], 1)
-            o["token"] = (own_sem[q], count[q])
+            o["token"] = (own_sem[q], done[q])
     g.wait_ge(T.sem.sent, sent[0])
     for name in ("oy0", "oy1", "oys"):
         g.sync.wait_ge(T.sem[name], 16)

@@ -3,13 +3,15 @@ from concourse.mybir import AluOpType, ActivationFunctionType
 
 RO = 3
 OPT = {
-    "clamp_s": (),
-    "fused": ((4, 5), (4, 5), (4, 5)),
-    "pieces": {7: ((0, 256), (256, 512))},
-    "hold_clamp": {"s": 150}, "hold_steps": {}, "wake": 200,
-    "land": 5.5, "start": 6.0,
-    "forward": ((True, True), (True, True), (True, True)),
+    "fused": ((0, 4, 5), (0, 4, 5), (0, 4, 5)),
+    "pieces": {0: ((0, 128), (128, 256), (256, 384), (384, 512)), 7: ((0, 256), (256, 512))},
+    "clamp_s": (), "kinds": (0, 128), "late": 8, "hold_last": {}, "hold_clamp": {}, "hold_mul": ({}, {}, {}), "hold_steps": ({}, {"v": 150}), "pick": 1.56, "again": False, "wake": 240,
+    "land": {"far0": 4.0, "far1": 3.0, "far2": 3.0, "near": 1.5},
+    "send": (((0, 2), (2, 4)), ((0, 2), (2, 4)), ((0, 2), (2, 4))),
+    "hand": (((0, 2), (2, 4)), ((0, 2), (2, 4)), ((0, 2), (2, 4))),
+    "calls": 2,
 }
+BIG = 1.5 * 2.0 ** 23
 PAD = 136
 RESIDENT = {3: "pw0", 7: "pw1"}
 IN_SBUF = {0: 0, 1: 1, 2: 2, 4: 3, 5: 4, 6: 5}
@@ -22,25 +24,26 @@ SCRATCH = {
     "off": ("sbuf", [128, 256], "uint16"),
     "sri": ("sbuf", [128, 256], "int32"), "wti": ("sbuf", [128, 256], "int32"), "bsi": ("sbuf", [128, 512], "int32"),
     "wtb": ("sbuf", [128, 256], "bfloat16"), "bsh": ("sbuf", [128, 512], "float16"),
-    "kc": ("sbuf", [128, 16], "float32"), "n128": ("sbuf", [128, 128], "bfloat16"),
+    "kc": ("sbuf", [128, 16], "float32"), "num": ("sbuf", [128, 160], "bfloat16"),
     "m16": ("sbuf", [128, 128], "bfloat16"), "lf": ("sbuf", [128, 32], "float32"),
     "zh": ("sbuf", [128, 256], "float16"), "neg": ("sbuf", [128, 512], "bfloat16"),
     "ki": ("sbuf", [128, 16], "int32"), "kj": ("sbuf", [128, 8], "int32"),
-    "rf": ("sbuf", [128, 8], "float32"), "rs": ("sbuf", [128, 16], "float32"),
+    "rf": ("sbuf", [128, 8], "float32"), "rs": ("sbuf", [128, 24], "float32"),
     "lst": ("sbuf", [128, 32], "uint16"),
-    "sel": ("sbuf", [128, 2048], "bfloat16"), "mov": ("sbuf", [128, 512], "float16"),
-    "fin": ("sbuf", [128, 512], "float16"), "idf": ("sbuf", [128, 512], "float32"),
+    "sel": ("sbuf", [128, 2048], "bfloat16"), "mov": ("sbuf", [128, 640], "float16"),
+    "fin": ("sbuf", [128, 640], "float16"), "idf": ("sbuf", [128, 512], "float32"),
     "idb": ("sbuf", [128, 128], "bfloat16"), "idh": ("sbuf", [128, 128], "float16"),
     "idn": ("sbuf", [128, 128], "float16"),
     "e8": ("sbuf", [128, 128], "float16"), "grp": ("sbuf", [128, 16], "float32"),
     "one": ("sbuf", [128, 128], "bfloat16"), "tie": ("sbuf", [128, 256], "bfloat16"),
-    "src": ("sbuf", [128, 256], "float32"), "seed": ("sbuf", [128, 128], "bfloat16"),
+    "src": ("sbuf", [128, 256], "float32"),
     "mid": ("sbuf", [128, 256], "bfloat16"), "kn": ("sbuf", [128, 64], "float32"),
-    "d1": ("sbuf", [128, 256], "bfloat16"),
+    "d1": ("sbuf", [128, 128], "bfloat16"),
     "z0": ("sbuf", [128, 256], "float32"), "z1": ("sbuf", [128, 256], "float32"),
     "mx": ("sbuf", [128, 512], "float32"), "nq": ("sbuf", [128, 512], "float16"),
     "sc": ("sbuf", [128, 512], "float32"),
-    "zi": ("sbuf", [128, 64], "int32"), "nw": ("sbuf", [128, 64], "int32"),
+    "zi": ("sbuf", [128, 64], "int32"), "less": ("sbuf", [128, 64], "bfloat16"),
+    "idp": ("sbuf", [128, 128], "float16"),
     "inj": ("sbuf", [128, 512], "float16"), "dd": ("sbuf", [128, 4 * PAD], "float16"),
     "pw0": ("psum", [128, 16, 32], "float32"), "pw1": ("psum", [128, 16, 32], "float32"),
     "px0": ("psum", [128, 512], "float32"), "px1": ("psum", [128, 512], "float32"),
@@ -48,7 +51,7 @@ SCRATCH = {
     "lu0": ("psum", [128, 512], "float32"), "lu1": ("psum", [128, 512], "float32"),
 }
 SEMAPHORES = (["cv", "cs", "ct", "cg", "sent", "la0", "la1", "lsr", "lwt", "lbs", "oy0", "oy1", "oys"]
-              + ["far%d%d" % (r, h) for r in range(RO) for h in range(2)] + ["near%d" % r for r in range(RO)])
+              + ["far%d%d" % (r, a) for r in range(RO) for a, b in OPT["send"][r]] + ["near%d" % r for r in range(RO)])
 
 A = AluOpType
 COPY = ActivationFunctionType.Copy
@@ -64,7 +67,6 @@ def rank_program(g, core, T, topo):
     own_sem = {"v": "cv", "s": "cs", "t": "ct", "g": "cg"}
     ops = []
     hold = [{}]
-    fwd = OPT["forward"]
 
     def w(name, a=0, b=None, st=1, rows=128):
         if b is None:
@@ -119,7 +121,7 @@ def rank_program(g, core, T, topo):
             return 300
         n = count(writes[0])
         if any(isinstance(x, tuple) and len(x) == 4 for x in reads):
-            return 70 + 1.56 * n
+            return 70 + OPT["pick"] * n
         if q == "v" and both and not any(psum(x[0]) for x in full):
             n *= 2
         if q == "v" and not any(wide(x) for x in full + writes):
@@ -155,7 +157,7 @@ def rank_program(g, core, T, topo):
         op("v", lambda: g.vector.transpose(out[1], a[1]), [a], [out])
 
     def act(out, a, scale=1.0, ext=(), f=COPY, bias=0.0):
-        op("s", lambda: g.scalar.activation(out[1], a[1], f, bias=bias, scale=scale), [a], [out], ext)
+        op("s", lambda: g.scalar.activation(out[1], a[1], f, bias=val(bias), scale=scale), [a, bias], [out], ext)
 
     def mm(out, l, r, start=True, stop=True):
         op("t", lambda: g.tensor.matmul(out[1], l[1], r[1], start, stop), [l, r], [out])
@@ -175,7 +177,6 @@ def rank_program(g, core, T, topo):
     far_die = [c for c in far if topo.die(c) == topo.die(core)]
     e_far = topo.engines(core, far[0])
     e_near = [e for e in topo.engines(core, near) if e not in e_far]
-    half = len(e_near) // 2
     sent = [0]
 
     def mask(es):
@@ -188,56 +189,60 @@ def rank_program(g, core, T, topo):
         rid, pid, _ = topo.addr(c)
         return DstId(rid=rid, pnc=pid)
 
-    def block(r, c, h):
-        a = T.rank_of(c) * 512 + h * 256
-        return w("tab%d" % r, a, a + 256)
+    def block(r, c, a, b):
+        return w("tab%d" % r, T.rank_of(c) * 512 + a * 128, T.rank_of(c) * 512 + b * 128)
 
-    hand_on = [[(far_die[0], e_near[:half]), (far_die[1], e_near[half:])], [(far_die[2], e_near)]]
+    def hand_on(b):
+        es = e_near + e_far if b == 4 else e_near
+        n = len(es) // 2
+        if b == 4 and OPT["calls"] == 1:
+            return [[(far_die[0], es[:n]), (far_die[1], es[n:n + n // 2]), (far_die[2], es[n + n // 2:])]]
+        return [[(far_die[0], es[:n]), (far_die[1], es[n:])], [(far_die[2], es)]]
 
-    def far_count(r, h):
-        return len(e_far) * len(far_die if fwd[r][h] else far)
+    def takers(r, a):
+        return far_die if any(x <= a < y for x, y in OPT["hand"][r]) else far
 
     def near_count(r):
-        return ((1 if r == 0 else 2) + 2 * sum(fwd[r])) * len(e_near)
+        return ((len(OPT["send"][r]) if r else 1) * len(e_near)
+                + sum(len(es) for a, b in OPT["hand"][r] for call in hand_on(b) for c, es in call))
 
-    def send(r, b, h, to_far=True, to_near=True):
-        to = far_die if fwd[r][h] else far
-        tr = []
-        if to_far:
-            tr.append(RemoteDMATransfer(dst_ids=[dst(c) for c in to], dma_engine_mask=mask(e_far),
-                                        remote_sem=T.sem["far%d%d" % (r, h)], srcs=[b[1]], dsts=[b[1] for c in to]))
-            sent[0] += len(e_far)
-        if to_near:
-            tr.append(RemoteDMATransfer(dst_ids=[dst(near)], dma_engine_mask=mask(e_near),
-                                        remote_sem=T.sem["near%d" % r], srcs=[b[1]], dsts=[b[1]]))
-            sent[0] += len(e_near)
-        op("g", lambda: g.remote_dma_fused(tr, local_sem=T.sem.sent), [b], [], mute=True)
-        ops[-1]["sends"] = r
+    def to_far(r, a, b):
+        x = block(r, core, a, b)
+        sent[0] += len(e_far)
+        return RemoteDMATransfer(dst_ids=[dst(c) for c in takers(r, a)], dma_engine_mask=mask(e_far),
+                                 remote_sem=T.sem["far%d%d" % (r, a)], srcs=[x[1]],
+                                 dsts=[x[1] for c in takers(r, a)])
 
-    def forward_call(r, h, call):
-        tr = []
-        for c, es in call:
-            b = block(r, c, h)
-            tr.append(RemoteDMATransfer(dst_ids=[dst(near)], dma_engine_mask=mask(es),
-                                        remote_sem=T.sem["near%d" % r], srcs=[b[1]], dsts=[b[1]]))
-            sent[0] += len(es)
-        op("g", lambda: g.remote_dma_fused(tr, local_sem=T.sem.sent), [], [],
-           ext=[("far%d%d" % (r, h), far_count(r, h))], mute=True)
+    def to_near(r, c, a, b, es):
+        x = block(r, c, a, b)
+        sent[0] += len(es)
+        return RemoteDMATransfer(dst_ids=[dst(near)], dma_engine_mask=mask(es),
+                                 remote_sem=T.sem["near%d" % r], srcs=[x[1]], dsts=[x[1]])
+
+    def remote(tr, reads, ext=()):
+        op("g", lambda: g.remote_dma_fused(tr, local_sem=T.sem.sent), reads, [], ext=ext, mute=True)
+
+    def send(r, a, b):
+        remote([to_far(r, a, b)] + ([to_near(r, core, a, b, e_near)] if r else []), [block(r, core, a, b)])
+        ops[-1]["sends"] = "far%d%d" % (r, a)
+
+    def arrivals(r, a, b):
+        return [("far%d%d" % (r, x), len(e_far) * len(takers(r, x))) for x, y in OPT["send"][r] if a <= x < b]
 
     def forward(r):
-        for h in range(2):
-            if fwd[r][h]:
-                for call in hand_on:
-                    forward_call(r, h, call)
+        for a, b in OPT["hand"][r]:
+            for call in hand_on(b):
+                remote([to_near(r, c, a, b, es) for c, es in call], [], arrivals(r, a, b))
+                ops[-1]["sends"] = "near%d" % r
 
     def landed(r):
-        return [("far%d0" % r, far_count(r, 0)), ("far%d1" % r, far_count(r, 1)), ("near%d" % r, near_count(r))]
+        return arrivals(r, 0, 4) + [("near%d" % r, near_count(r))]
 
     px, pk, lu = ["px0", "px1"], ["pk0", "pk1"], ["lu0", "lu1"]
     L_A, L_B = 0, 16
 
-    load("y", block(0, core, 0), T.a0[:, 0:256], "la0")
-    load("s", block(0, core, 1), T.a0[:, 256:512], "la1")
+    load("y", block(0, core, 0, 2), T.a0[:, 0:256], "la0")
+    load("s", block(0, core, 2, 4), T.a0[:, 256:512], "la1")
     load("y", w("sri"), T.sr[:, :], "lsr")
     load("s", w("wti"), T.wt[:, :], "lwt")
     load("y", w("bsi", rows=8), T.bs[:, :], "lbs")
@@ -245,53 +250,54 @@ def rank_program(g, core, T, topo):
     iota(w("kc"), [[-1, 16]], 0, 1)
     iota(w("m16"), [[16, 8], [0, 16]], 0, 0)
     iota(w("lf", L_A, L_A + 16), [[1, 8], [16, 2]], 0, 0)
-    iota(w("lf", L_B, L_B + 16), [[16, 2], [32, 8]], 0, 0)
-    iota(w("n128"), [[1, 128]], 0, 0)
-    send(0, block(0, core, 0), 0, to_near=False)
-    send(0, block(0, core, 1), 1, to_near=False)
-    send(0, w("tab0", rank * 512, rank * 512 + 512), 0, to_far=False)
+    iota(w("lf", L_B, L_B + 16), [[16, 2], [1, 2], [64, 4]], 0, 0)
+    iota(w("num"), [[1, 160]], 0, 0)
+    for a, b in OPT["send"][0]:
+        send(0, a, b)
+    remote([to_near(0, core, 0, 4, e_near)], [block(0, core, 0, 4)])
     forward(0)
 
     k = w("kc", 0, 1)
+    n128 = w("num", 0, 128)
     cp(w("ki"), w("kc"))
-    FIELDS = ((0, 15), (3, 1), (0, 7), (4, 7), (4, 1), (5, 3))
+    FIELDS = ((3, 1), (0, 7), (4, 7), (3, 3), (5, 3))
     for n, (shift, bits) in enumerate(FIELDS):
         ts(w("kj", n, n + 1), w("ki", 0, 1), shift, bits, A.arith_shift_right, A.bitwise_and)
     cp(w("rf", 0, len(FIELDS)), w("kj", 0, len(FIELDS)))
-    low4, bit3, low3, group, bit4, top2 = [w("rf", n, n + 1) for n in range(len(FIELDS))]
+    bit3, low3, group, mid2, top2 = [w("rf", n, n + 1) for n in range(len(FIELDS))]
 
-    def col(n):
-        return w("rs", n, n + 1)
+    def col(n, m=1):
+        return w("rs", n, n + m)
 
     ts(col(0), bit3, 8.0, None, A.mult)
     ts(col(1), low3, 32.0, None, A.mult)
+    ts(col(2), bit3, 32.0, None, A.mult)
+    ts(col(3), low3, 2.0, None, A.mult)
     ts(w("lst", L_A, L_A + 16), w("lf", L_A, L_A + 16), col(0), col(1), A.add, A.add)
-    ts(w("lst", L_B, L_B + 16), w("lf", L_B, L_B + 16), low4, None, A.add)
+    ts(w("lst", L_B, L_B + 16), w("lf", L_B, L_B + 16), col(2), col(3), A.add, A.add)
     for t in range(16):
         ts(w("sel", t * 128, t * 128 + 128), w("m16"), w("kc", t, t + 1), None, A.is_equal)
 
     def mov(to, frm):
-        a = (to * 2 + frm) * 128
+        a = frm * 160 + 24 - 8 * to
         return w("mov", a, a + 128)
 
     def fin(to, frm):
-        a = (to * 2 + frm) * 128
+        a = frm * 160 + 3 - to
         return w("fin", a, a + 128)
 
     def idf(n):
         return w("idf", n * 128, n * 128 + 128)
 
-    ts(col(2), bit4, 1000.0, k, A.mult, A.add)
-    ts(col(3), bit4, -1000.0, k, A.mult, A.add)
-    for to in range(2):
-        ts(mov(to, 0), w("n128"), col(2), 16.0 * to, A.subtract, A.is_equal)
-        ts(mov(to, 1), w("n128"), col(3), 16.0 * to + 984.0, A.subtract, A.is_equal)
+    ts(col(12, 4), w("num", 0, 4), mid2, 1000.0, A.not_equal, A.mult)
+    ts(col(16, 4), col(12, 4), k, None, A.add)
+    for frm in range(4):
+        ts(w("mov", frm * 160, frm * 160 + 160), w("num"), col(16 + frm), 24.0 - 8 * frm, A.subtract, A.is_equal)
     fill(w("one", rows=32), 1.0)
     for s in range(8):
-        act(w("tie", s, 256, 8, rows=1), w("one", 0, 32, rows=1), scale=float(7 - s))
-    act(w("seed", rows=1), w("tie", 0, 128, rows=1), scale=4096.0, f=IDENT, bias=2048.0)
-    ts(w("idb"), w("n128"), k, None, A.is_equal)
-    ts(w("idh"), w("n128"), k, None, A.is_equal)
+        act(w("tie", s, 256, 8, rows=1), w("one", 0, 32, rows=1), scale=3.5 - s)
+    ts(w("idb"), n128, k, None, A.is_equal)
+    ts(w("idh"), n128, k, None, A.is_equal)
     ts(w("e8", rows=8), w("m16", rows=8), 0.0625, w("kc", 0, 1, rows=8), A.mult, A.is_equal)
 
     def weights(bank, chunk):
@@ -307,53 +313,53 @@ def rank_program(g, core, T, topo):
         return w("wsb", IN_SBUF[c] * 512 + a, IN_SBUF[c] * 512 + b)
 
     cp(w("z0"), ind(w("sri"), w("lst", L_A, L_A + 16)))
-    for b in range(2):
-        cp(w("wtb", b, 256, 2), w("wti", b * 128, b * 128 + 128))
+    cp(w("wtb"), w("wti"))
     for c, bank in ((4, "px0"), (0, "px1"), (5, "pk0"), (1, "pk1")):
         weights(bank, c)
         act(wt(c), w(bank))
     turn(w("z1"), w("z0"))
     ts(w("zh"), ind(w("z1"), w("lst", L_B, L_B + 16)), -2048.0, None, A.add)
     for h in range(2):
-        for g0 in range(2):
-            mm(w(lu[h], 0, 128), mov(g0, h), w("zh", g0 * 128, g0 * 128 + 128), g0 == 0, g0 == 1)
+        for m6 in range(2):
+            for to in range(4):
+                mm(w(lu[h], m6 * 64, m6 * 64 + 64), mov(to, 2 * h + m6), w("zh", to * 64, to * 64 + 64),
+                   to == 0, to == 3)
         ts(w("off", h * 128, h * 128 + 128), w(lu[h], 0, 128), 2048.0, None, A.add)
-    for h in range(2):
-        for b in range(2):
-            cp(w("bsh", h * 256 + b, h * 256 + 256, 2, rows=8),
-               w("bsi", h * 256 + b * 128, h * 256 + b * 128 + 128, rows=8))
-    for c, bank in ((2, "px0"), (6, "px1")):
-        weights(bank, c)
-        cp(wt(c), w(bank))
+    cp(w("bsh", rows=8), w("bsi", rows=8))
+    weights("px0", 2)
+    cp(wt(2), w("px0"))
+    weights("px1", 6)
+    act(wt(6), w("px1"))
     for c in RESIDENT:
         weights(RESIDENT[c], c)
-    for h in range(2):
-        mm(w(lu[h], 128, 256), w("one", rows=1), w("seed", rows=1), True, False)
-        for g0 in range(2):
-            mm(w(lu[h], 128, 256), w("zh", g0 * 128, g0 * 128 + 128), mov(g0, h), False, g0 == 1)
+    ts(col(9), low3, -4096.0, 7 * 4096.0 + 2048.0, A.mult, A.add)
+    for n, c in enumerate((1.0, 1.0 / 4096, 13.0 / 4096, 7.0 / 4096)):
+        act(idf(n), w("idb"), scale=c)
 
     def late_constants():
-        ts(w("grp", 0, 8), w("n128", 0, 8), group, -8.0, A.is_equal, A.mult)
-        ts(w("grp", 8, 16), w("n128", 0, 8), group, 8.0, A.is_equal, A.mult)
+        ts(w("grp", 0, 8), w("num", 0, 8), group, -8.0, A.is_equal, A.mult)
+        ts(w("grp", 8, 16), w("num", 0, 8), group, 8.0, A.is_equal, A.mult)
         fill(w("d1"), 0.0)
-        fill(w("d1", 0, 256, 8), -3.0e7)
-        fill(w("kn"), 0.0)
+        fill(w("d1", 0, 128, 8), -3.0e7)
         fill(w("inj"), 0.0)
         fill(w("dd", 128, 4 * PAD, PAD), 0.0)
-        ts(w("idn"), w("n128"), k, -1.0, A.is_equal, A.mult)
+        fill(w("less", 0, 16, rows=32), 0.0)
+        fill(w("less", 16, 32, rows=32), -BIG / 4096)
+        fill(w("less", 32, 64, rows=32), 0.5)
+        ts(w("idn"), n128, k, -4096.0, A.is_equal, A.mult)
+        ts(w("idp"), n128, k, 4096.0, A.is_equal, A.mult)
         ts(col(4), low3, 4096.0, -7 * 4096.0, A.mult, A.add)
-        for n, c in enumerate((1.0, 8.0, 104.0, 56.0)):
-            act(idf(n), w("idb"), scale=c)
         act(w("mid", rows=1), w("tie", rows=1), scale=0.0, f=IDENT, bias=2048.0)
-        ts(col(5), top2, 32.0, bit3, A.mult, A.add)
-        ts(col(6), low3, 4.0, col(5), A.mult, A.add)
-        ts(col(7), bit4, 1000.0, col(6), A.mult, A.add)
-        ts(col(8), bit4, -1000.0, col(6), A.mult, A.add)
-        for to in range(2):
-            ts(fin(to, 0), w("n128"), col(7), 2.0 * to, A.subtract, A.is_equal)
-            ts(fin(to, 1), w("n128"), col(8), 2.0 * to + 1000.0, A.subtract, A.is_equal)
 
-    signs = (("idn", "idh"), ("idh", "idn"))
+    def last_constants():
+        ts(col(5), top2, 32.0, None, A.mult)
+        ops[-1]["ext"] = landed(1)
+        ts(col(6), low3, 4.0, col(5), A.mult, A.add)
+        ts(col(20, 4), col(12, 4), col(6), None, A.add)
+        for frm in range(4):
+            ts(w("fin", frm * 160, frm * 160 + 136), w("num", 0, 136), col(20 + frm), 3.0, A.subtract, A.is_equal)
+
+    signs = (("idn", "idp"), ("idp", "idn"))
 
     def put(h, blk):
         a = h * 256 + blk * 128
@@ -365,29 +371,29 @@ def rank_program(g, core, T, topo):
 
     def sources(r, h):
         src = w("src", h * 128, h * 128 + 128)
-        if r:
-            mm(w(lu[h], 128, 256), idf(0), src, True, False)
-            terms = put(h, 0) + put(h, 1) + carried(h, 0) + carried(h, 1)
-            for n, (x, sign) in enumerate(terms):
-                mm(w(lu[h], 128, 256), w(sign), x, False, n == len(terms) - 1)
-        act(src, w(lu[h], 128, 256))
-        mm(w(lu[h], 0, 128), src, idf(0), True, False)
+        act(src, w(lu[h], 0, 128), f=IDENT, bias=0.0 if r else col(9))
+        mm(w(pk[h], 256, 384), src, idf(0))
+        mm(w(lu[h], 0, 128), idf(0), src, True, False)
 
     def choose(r, h):
         a, n = h * 256, h * 32
-        src = w("src", h * 128, h * 128 + 128)
-        scan(w("mx", a, a + 256), w("d1"), w(pk[h], 0, 256), A.add, A.max)
-        act(w("kn", n + 16, n + 30), w("mx", a + 128 + 23, a + 256, 8))
-        act(w("kn", n + 30, n + 32), w("mx", a + 128 + 7, a + 128 + 16, 8))
-        tt(w("nq", a, a + 256), w(pk[h], 0, 256), w("mx", a, a + 256), A.not_equal)
+        src = w(pk[h], 256, 384)
+        for c in OPT["kinds"]:
+            scan(w("mx", a + c, a + c + 128), w("d1"), w(pk[h], c, c + 128), A.add, A.max)
+        act(w("kn", n, n + 14), w("mx", a + 128 + 23, a + 256, 8), 0.125, f=IDENT, bias=BIG)
+        act(w("kn", n + 14, n + 16), w("mx", a + 128 + 7, a + 128 + 16, 8), 0.125, f=IDENT, bias=BIG)
+        mm(w(px[h], 0, 32), w("one", rows=1), w("less", 0, 32, rows=1), True, False)
+        mm(w(px[h], 16, 32), idf(1), w("kn", n, n + 16), False, False)
+        mm(w(px[h], 0, 32), w("one", rows=1), w("less", 32, 64, rows=1), False, False)
+        for c in (0, 128):
+            tt(w("nq", a + c, a + c + 128), w(pk[h], c, c + 128), w("mx", a + c, a + c + 128), A.not_equal)
         scan(w("sc", a, a + 128), w("nq", a, a + 128), src, A.mult, A.max)
-        mm(w(px[h], 0, 16), idf(1), w("sc", a + 7, a + 128, 8))
-        mm(w(px[h], 16, 32), idf(3), w("sc", a + 7, a + 128, 8), True, False)
+        mm(w(px[h], 0, 16), idf(1), w("sc", a + 7, a + 128, 8), False, False)
+        mm(w(px[h], 16, 32), idf(3), w("sc", a + 7, a + 128, 8), False, False)
         scan(w("sc", a + 128, a + 256), w("nq", a + 128, a + 256), src, A.mult, A.max)
         mm(w(px[h], 16, 32), idf(2), w("sc", a + 128 + 7, a + 256, 8), False, True)
-        tt(w("zi", n, n + 32), w(px[h], 0, 32), w("kn", n, n + 32), A.add)
-        ts(w("nw", n, n + 32), w("zi", n, n + 32), 3, 4095, A.arith_shift_right, A.bitwise_and)
-        ts(w("inj", a + 7, a + 256, 8), w("nw", n, n + 32), -2048.0, None, A.add)
+        ts(w("zi", n, n + 32), w(px[h], 0, 32), 1.0 + 2.0 ** -22, None, A.mult)
+        tt(w("inj", a + 7, a + 256, 8), w(px[h], 0, 32), w("zi", n, n + 32), A.subtract)
         for x, sign in put(h, 0) + put(h, 1):
             mm(w(lu[h], 0, 128), x, w(sign), False, False)
         for blk in range(2):
@@ -398,23 +404,25 @@ def rank_program(g, core, T, topo):
                 mm(w(lu[h], 0, 128), x, w(sign), False, blk == 1 and m == 1)
         if r < RO - 1:
             ts(w("off", h * 128, h * 128 + 128), w(lu[h], 0, 128), col(4), None, A.add)
-        else:
-            ts(w("zh", h * 128, h * 128 + 128), w(lu[h], 0, 128), col(4), -2048.0, A.add, A.add)
-            if h == 0:
-                mm(w3("pw0", 0, 8), w("one", rows=1), w("mid", rows=1), True, False)
-            for g0 in range(2):
-                mm(w3("pw0", 0, 8, g0 * 16, g0 * 16 + 16), fin(h, g0), w("zh", h * 128, h * 128 + 128),
-                   False, h == 1 and g0 == 1)
+
+    def unlist(h):
+        ts(w("zh", h * 128, h * 128 + 128), w(lu[h], 0, 128), col(4), -2048.0, A.add, A.add)
+        for m6 in range(2):
+            for frm in range(4):
+                c = frm // 2 * 16
+                mm(w3("pw0", 0, 8, c + frm % 2, c + 16, 2), fin(2 * h + m6, frm),
+                   w("zh", h * 128 + m6 * 64, h * 128 + m6 * 64 + 64), False, (h, m6, frm) == (1, 1, 3))
 
     for r in range(RO):
         last = r == RO - 1
         tab = w("tab%d" % r)
         arrived = landed(r)
 
-        def new_a(h, a=0, b=256):
-            if last:
-                return w("aout", h * 256 + a, h * 256 + b)
-            return w("tab%d" % (r + 1), rank * 512 + h * 256 + a, rank * 512 + h * 256 + b)
+        def new_a(a, b):
+            return w("aout", a * 128, b * 128) if last else block(r + 1, core, a, b)
+
+        def sums(qt, a=0, b=128):
+            return w(pk[qt // 2], 384 + a, 384 + b) if qt % 2 else w(px[qt // 2], a, b)
 
         def picked(c, a, b):
             return ind(tab, w("off", c * 32 + a // 16, c * 32 + b // 16))
@@ -429,26 +437,24 @@ def rank_program(g, core, T, topo):
             tt(w("wp", c * 512 + a, c * 512 + b), w("p", c * 512 + a, c * 512 + b), wt(c, a, b), A.mult)
 
         def wires(c):
-            a = c % 4 * 64
+            a = c % 2 * 64
             for s in range(8):
-                mm(w(px[c // 4], a, a + 64), w("idh"), w("wp", c * 512 + s, c * 512 + 512, 8),
-                   False, c % 4 == 3 and s == 7)
+                mm(sums(c // 2, a, a + 64), w("idh"), w("wp", c * 512 + s, c * 512 + 512, 8),
+                   False, c % 2 == 1 and s == 7)
 
-        def clamp(h):
-            if h in OPT["clamp_s"]:
-                act(w("neg", h * 256, h * 256 + 256), w(px[h], 0, 256), -1.0, f=RELU, bias=255.0)
-            for b in range(2):
-                if h in OPT["clamp_s"]:
-                    act(new_a(h, b * 128, b * 128 + 128), w("neg", h * 256 + b, h * 256 + 256, 2), -1.0,
-                        f=RELU, bias=255.0)
-                else:
-                    ts(new_a(h, b * 128, b * 128 + 128), w(px[h], b, 256, 2), 0.0, 255.0, A.max, A.min)
-            if last:
-                store("y", T.ya[:, h * 256:h * 256 + 256], new_a(h), "oy%d" % h)
+        def clamp(qt):
+            if qt in OPT["clamp_s"]:
+                act(w("neg", qt * 128, qt * 128 + 128), sums(qt), -1.0, f=RELU, bias=255.0)
+                act(new_a(qt, qt + 1), w("neg", qt * 128, qt * 128 + 128), -1.0, f=RELU, bias=255.0)
             else:
-                send(r + 1, new_a(h), h)
-            for b in range(2):
-                mm(w(px[h], 256 + b, 512, 2), w("idb"), new_a(h, b * 128, b * 128 + 128))
+                ts(new_a(qt, qt + 1), sums(qt), 0.0, 255.0, A.max, A.min)
+            if last and qt % 2:
+                store("y", T.ya[:, qt // 2 * 256:qt // 2 * 256 + 256], new_a(qt - 1, qt + 1), "oy%d" % (qt // 2))
+            for a, b in () if last else OPT["send"][r + 1]:
+                if b == qt + 1:
+                    send(r + 1, a, b)
+            c = 256 + qt % 2 * 128
+            mm(w(px[qt // 2], c, c + 128), w("idb"), new_a(qt, qt + 1))
 
         def score(h, s):
             a = (h * 8 + s) * 256
@@ -456,22 +462,34 @@ def rank_program(g, core, T, topo):
             for b in range(2):
                 mm(w(pk[h], b * 8 + s, 256, 16), w("q", a + b, a + 256, 2), w("grp"), False, s == 7 and b == 1)
 
-        for h in range(2):
-            mm(w(px[h], 0, 256), w("e8", rows=8), w("bsh", h * 256, h * 256 + 256, rows=8), True, False)
-            for c in range(4 * h, 4 * h + 4):
+        def again(h):
+            for c in OPT["fused"][r]:
+                if c // 4 == h:
+                    gather(c, 0, 256)
+                    gather(c, 256, 512)
+
+        for qt in range(4):
+            if qt % 2:
+                sources(r, qt // 2)
+            mm(sums(qt), w("e8", rows=8), w("bsh", qt * 128, qt * 128 + 128, rows=8), True, False)
+            for c in range(2 * qt, 2 * qt + 2):
                 for a, b in OPT["pieces"].get(c, ((0, 512),)):
                     if c in OPT["fused"][r]:
                         gather_mul(c, a, b)
                     else:
+                        hold[0] = OPT["hold_mul"][r]
                         gather(c, a, b)
                         mul(c, a, b)
+                        hold[0] = {}
                 wires(c)
             hold[0] = OPT["hold_clamp"]
-            clamp(h)
+            clamp(qt)
             hold[0] = {}
-        for c in OPT["fused"][r]:
-            gather(c, 0, 256)
-            gather(c, 256, 512)
+            if qt == 1 and OPT["again"]:
+                again(0)
+        if not OPT["again"]:
+            again(0)
+        again(1)
         if not last:
             forward(r + 1)
         if r == 0:
@@ -479,11 +497,24 @@ def rank_program(g, core, T, topo):
         for h in range(2):
             mm(w(pk[h], 0, 256), w("one", rows=1), w("tie", rows=1), True, False)
             for s in range(8):
+                if last and h == 1 and s == OPT["late"]:
+                    choose(r, 0)
                 score(h, s)
-            sources(r, h)
-            hold[0] = OPT["hold_steps"]
-            choose(r, h)
+            if not last:
+                hold[0] = OPT["hold_steps"][h]
+                choose(r, h)
+                hold[0] = {}
+        if r == 1:
+            last_constants()
+        if last:
+            mm(w3("pw0", 0, 8), w("one", rows=1), w("mid", rows=1), True, False)
+            hold[0] = OPT["hold_last"]
+            choose(r, 1)
             hold[0] = {}
+            if OPT["late"] == 8:
+                choose(r, 0)
+            for h in range(2):
+                unlist(h)
     for x in range(8):
         turn(w("z0", x, 256, 8), w3("pw0", x, x + 1))
     store("y", T.ys[:, :], w("z0"), "oys")
@@ -496,21 +527,21 @@ def rank_program(g, core, T, topo):
             for views, writing in ((o["r"], False), (o["w"], True)):
                 for name, _, bits in views:
                     for m, mbits, mw in seen.get(name, []):
-                        if (mw or writing) and (psum(name) or mbits & bits) and not ops[m]["mute"]:
+                        if (psum(name) and (mw or writing or ops[m]["q"] != o["q"])
+                                or (mw or writing) and mbits & bits and not ops[m]["mute"]):
                             both_t = ops[m]["q"] == "t" and o["q"] == "t"
                             before[n][m] = DMA if ops[m]["dma"] else 0 if both_t else WAKE
             for views, writing in ((o["r"], False), (o["w"], True)):
                 for name, _, bits in views:
                     seen.setdefault(name, []).append((n, bits, writing))
-            if o["q"] in "gy" or o["dma"]:
+            if o["dma"]:
                 if o["q"] in last_of:
                     before[n].setdefault(last_of[o["q"]], 0)
                 last_of[o["q"]] = n
+            for name, _ in o["ext"]:
+                before[n][last_send[name]] = OPT["land"][name[:-1]] / 0.83e-3
             if "sends" in o:
                 last_send[o["sends"]] = n
-            elif o["ext"] and o["q"] != "g":
-                r = int(o["ext"][0][0][3])
-                before[n][last_send[r]] = (OPT["land"] if r else OPT["start"]) / 0.83e-3
         after = [[] for _ in ops]
         for n, b in enumerate(before):
             for m in b:

from concourse.bass import DstId, RemoteDMATransfer
from concourse.mybir import AluOpType, ActivationFunctionType

RO = 3
OPT = {
    "fused": ((0, 4, 5), (0, 4, 5), (0, 4, 5)),
    "pieces": {0: ((0, 128), (128, 256), (256, 384), (384, 512)), 7: ((0, 256), (256, 512))},
    "clamp_s": (), "kinds": (0, 128), "late": 8, "hold_last": {}, "hold_clamp": {}, "hold_mul": ({}, {}, {}), "hold_steps": ({}, {"v": 150}), "pick": 1.56, "again": False, "wake": 240,
    "land": {"far0": 4.0, "far1": 3.0, "far2": 3.0, "near": 1.5},
    "send": (((0, 2), (2, 4)), ((0, 2), (2, 4)), ((0, 2), (2, 4))),
    "hand": (((0, 2), (2, 4)), ((0, 2), (2, 4)), ((0, 2), (2, 4))),
    "calls": 2,
}
BIG = 1.5 * 2.0 ** 23
PAD = 136
RESIDENT = {3: "pw0", 7: "pw1"}
IN_SBUF = {0: 0, 1: 1, 2: 2, 4: 3, 5: 4, 6: 5}

SCRATCH = {
    "tab0": ("sbuf", [128, 4096], "bfloat16"), "tab1": ("sbuf", [128, 4096], "bfloat16"),
    "tab2": ("sbuf", [128, 4096], "bfloat16"), "aout": ("sbuf", [128, 512], "bfloat16"),
    "p": ("sbuf", [128, 4096], "bfloat16"), "wp": ("sbuf", [128, 4096], "float16"),
    "q": ("sbuf", [128, 4096], "float32"), "wsb": ("sbuf", [128, 3072], "bfloat16"),
    "off": ("sbuf", [128, 256], "uint16"),
    "sri": ("sbuf", [128, 256], "int32"), "wti": ("sbuf", [128, 256], "int32"), "bsi": ("sbuf", [128, 512], "int32"),
    "wtb": ("sbuf", [128, 256], "bfloat16"), "bsh": ("sbuf", [128, 512], "float16"),
    "kc": ("sbuf", [128, 16], "float32"), "num": ("sbuf", [128, 160], "bfloat16"),
    "m16": ("sbuf", [128, 128], "bfloat16"), "lf": ("sbuf", [128, 32], "float32"),
    "zh": ("sbuf", [128, 256], "float16"), "neg": ("sbuf", [128, 512], "bfloat16"),
    "ki": ("sbuf", [128, 16], "int32"), "kj": ("sbuf", [128, 8], "int32"),
    "rf": ("sbuf", [128, 8], "float32"), "rs": ("sbuf", [128, 24], "float32"),
    "lst": ("sbuf", [128, 32], "uint16"),
    "sel": ("sbuf", [128, 2048], "bfloat16"), "mov": ("sbuf", [128, 640], "float16"),
    "fin": ("sbuf", [128, 640], "float16"), "idf": ("sbuf", [128, 512], "float32"),
    "idb": ("sbuf", [128, 128], "bfloat16"), "idh": ("sbuf", [128, 128], "float16"),
    "idn": ("sbuf", [128, 128], "float16"),
    "e8": ("sbuf", [128, 128], "float16"), "grp": ("sbuf", [128, 16], "float32"),
    "one": ("sbuf", [128, 128], "bfloat16"), "tie": ("sbuf", [128, 256], "bfloat16"),
    "src": ("sbuf", [128, 256], "float32"),
    "mid": ("sbuf", [128, 256], "bfloat16"), "kn": ("sbuf", [128, 64], "float32"),
    "d1": ("sbuf", [128, 128], "bfloat16"),
    "z0": ("sbuf", [128, 256], "float32"), "z1": ("sbuf", [128, 256], "float32"),
    "mx": ("sbuf", [128, 512], "float32"), "nq": ("sbuf", [128, 512], "float16"),
    "sc": ("sbuf", [128, 512], "float32"),
    "zi": ("sbuf", [128, 64], "int32"), "less": ("sbuf", [128, 64], "bfloat16"),
    "idp": ("sbuf", [128, 128], "float16"),
    "inj": ("sbuf", [128, 512], "float16"), "dd": ("sbuf", [128, 4 * PAD], "float16"),
    "pw0": ("psum", [128, 16, 32], "float32"), "pw1": ("psum", [128, 16, 32], "float32"),
    "px0": ("psum", [128, 512], "float32"), "px1": ("psum", [128, 512], "float32"),
    "pk0": ("psum", [128, 512], "float32"), "pk1": ("psum", [128, 512], "float32"),
    "lu0": ("psum", [128, 512], "float32"), "lu1": ("psum", [128, 512], "float32"),
}
SEMAPHORES = (["cv", "cs", "ct", "cg", "sent", "la0", "la1", "lsr", "lwt", "lbs", "oy0", "oy1", "oys"]
              + ["far%d%d" % (r, a) for r in range(RO) for a, b in OPT["send"][r]] + ["near%d" % r for r in range(RO)])

A = AluOpType
COPY = ActivationFunctionType.Copy
IDENT = ActivationFunctionType.Identity
RELU = ActivationFunctionType.Relu


def rank_program(g, core, T, topo):
    rank = T.rank_of(core)
    if rank is None:
        return
    queue = {"v": g.vector, "s": g.scalar, "t": g.tensor, "g": g, "y": g.sync}
    own_sem = {"v": "cv", "s": "cs", "t": "ct", "g": "cg"}
    ops = []
    hold = [{}]

    def w(name, a=0, b=None, st=1, rows=128):
        if b is None:
            b = SCRATCH[name][1][1]
        bits = 0
        if st == 1:
            bits = ((1 << (b - a)) - 1) << a
            ap = T[name][0:rows, a:b]
        elif st == -1:
            bits = ((1 << (b - a)) - 1) << a
            ap = T[name][0:rows, b - 1:a - 1:-1] if a else T[name][0:rows, b - 1::-1]
        else:
            for c in range(a, b, st):
                bits |= 1 << c
            ap = T[name][0:rows, a:b:st]
        return (name, ap, bits)

    def w3(name, a, b, c=0, d=32, st=1):
        bits = 0
        for x in range(a, b):
            for y in range(c, d, st):
                bits |= 1 << (x * 32 + y)
        return (name, T[name][:, a, c:d:st] if b == a + 1 else T[name][:, a:b, c:d:st], bits)

    def ind(win, lst):
        return ("", win[1].indirect(lst[1]), 0, [win, lst])

    def parts(x):
        if not isinstance(x, tuple):
            return []
        return x[3] if len(x) == 4 else [x]

    def val(x):
        return x[1] if isinstance(x, tuple) else x

    def psum(name):
        return SCRATCH[name][0] == "psum"

    def count(x):
        return bin(x[2]).count("1")

    def wide(x):
        return SCRATCH[x[0]][2] in ("float32", "int32")

    def cycles(q, reads, writes, both):
        full = [x for x in reads if isinstance(x, tuple) and len(x) == 3 and count(x) > 1]
        if q == "t":
            return max(min(64, count(reads[0])), count(reads[1])) * (4 if wide(reads[0]) else 1) / 2
        if q == "g" and writes:
            return 160 + 2 * count(writes[0])
        if q not in "vs" or not writes:
            return 300
        n = count(writes[0])
        if any(isinstance(x, tuple) and len(x) == 4 for x in reads):
            return 70 + OPT["pick"] * n
        if q == "v" and both and not any(psum(x[0]) for x in full):
            n *= 2
        if q == "v" and not any(wide(x) for x in full + writes):
            n /= 2
        return 12 + max(64, n)

    def op(q, fn, reads, writes, ext=(), dma=None, mute=False, both=False):
        rd = []
        for x in reads:
            rd += parts(x)
        ops.append({"q": q, "fn": fn, "r": rd, "w": list(writes), "ext": list(ext), "dma": dma, "mute": mute,
                    "hold": hold[0].get(q, 0), "cost": 80 if dma else cycles(q, reads, list(writes), both)})

    def tt(out, a, b, f, ext=()):
        op("v", lambda: g.vector.tensor_tensor(out[1], a[1], b[1], f), [a, b], [out], ext, both=True)

    def ts(out, a, s1, s2, f0, f1=None):
        if f1 is None:
            op("v", lambda: g.vector.tensor_scalar(out[1], a[1], val(s1), None, f0), [a, s1], [out])
        else:
            op("v", lambda: g.vector.tensor_scalar(out[1], a[1], val(s1), val(s2), f0, f1), [a, s1, s2], [out])

    def cp(out, a):
        op("v", lambda: g.vector.tensor_copy(out[1], a[1]), [a], [out])

    def fill(out, c):
        op("v", lambda: g.vector.memset(out[1], c), [], [out])

    def scan(out, a, b, f0, f1):
        op("v", lambda: g.vector.tensor_tensor_scan(out[1], a[1], b[1], 0.0, f0, f1), [a, b], [out])

    def turn(out, a):
        op("v", lambda: g.vector.transpose(out[1], a[1]), [a], [out])

    def act(out, a, scale=1.0, ext=(), f=COPY, bias=0.0):
        op("s", lambda: g.scalar.activation(out[1], a[1], f, bias=val(bias), scale=scale), [a, bias], [out], ext)

    def mm(out, l, r, start=True, stop=True):
        op("t", lambda: g.tensor.matmul(out[1], l[1], r[1], start, stop), [l, r], [out])

    def iota(out, pat, base, cm):
        op("g", lambda: g.iota(out[1], pat, base, cm, allow_small_or_imprecise_dtypes=True), [], [out])

    def load(q, out, src, sem):
        op(q, lambda: queue[q].dma_start(out[1], src), [], [out], dma=sem)

    def store(q, dst, a, sem):
        op(q, lambda: queue[q].dma_start(dst, a[1]), [a], [], dma=sem)

    cores = list(T.cores)
    near = [c for c in cores if c != core and topo.chip(c) == topo.chip(core)][0]
    far = [c for c in cores if topo.chip(c) != topo.chip(core)]
    far_die = [c for c in far if topo.die(c) == topo.die(core)]
    e_far = topo.engines(core, far[0])
    e_near = [e for e in topo.engines(core, near) if e not in e_far]
    sent = [0]

    def mask(es):
        m = 0
        for e in es:
            m |= 1 << e
        return m

    def dst(c):
        rid, pid, _ = topo.addr(c)
        return DstId(rid=rid, pnc=pid)

    def block(r, c, a, b):
        return w("tab%d" % r, T.rank_of(c) * 512 + a * 128, T.rank_of(c) * 512 + b * 128)

    def hand_on(b):
        es = e_near + e_far if b == 4 else e_near
        n = len(es) // 2
        if b == 4 and OPT["calls"] == 1:
            return [[(far_die[0], es[:n]), (far_die[1], es[n:n + n // 2]), (far_die[2], es[n + n // 2:])]]
        return [[(far_die[0], es[:n]), (far_die[1], es[n:])], [(far_die[2], es)]]

    def takers(r, a):
        return far_die if any(x <= a < y for x, y in OPT["hand"][r]) else far

    def near_count(r):
        return ((len(OPT["send"][r]) if r else 1) * len(e_near)
                + sum(len(es) for a, b in OPT["hand"][r] for call in hand_on(b) for c, es in call))

    def to_far(r, a, b):
        x = block(r, core, a, b)
        sent[0] += len(e_far)
        return RemoteDMATransfer(dst_ids=[dst(c) for c in takers(r, a)], dma_engine_mask=mask(e_far),
                                 remote_sem=T.sem["far%d%d" % (r, a)], srcs=[x[1]],
                                 dsts=[x[1] for c in takers(r, a)])

    def to_near(r, c, a, b, es):
        x = block(r, c, a, b)
        sent[0] += len(es)
        return RemoteDMATransfer(dst_ids=[dst(near)], dma_engine_mask=mask(es),
                                 remote_sem=T.sem["near%d" % r], srcs=[x[1]], dsts=[x[1]])

    def remote(tr, reads, ext=()):
        op("g", lambda: g.remote_dma_fused(tr, local_sem=T.sem.sent), reads, [], ext=ext, mute=True)

    def send(r, a, b):
        remote([to_far(r, a, b)] + ([to_near(r, core, a, b, e_near)] if r else []), [block(r, core, a, b)])
        ops[-1]["sends"] = "far%d%d" % (r, a)

    def arrivals(r, a, b):
        return [("far%d%d" % (r, x), len(e_far) * len(takers(r, x))) for x, y in OPT["send"][r] if a <= x < b]

    def forward(r):
        for a, b in OPT["hand"][r]:
            for call in hand_on(b):
                remote([to_near(r, c, a, b, es) for c, es in call], [], arrivals(r, a, b))
                ops[-1]["sends"] = "near%d" % r

    def landed(r):
        return arrivals(r, 0, 4) + [("near%d" % r, near_count(r))]

    px, pk, lu = ["px0", "px1"], ["pk0", "pk1"], ["lu0", "lu1"]
    L_A, L_B = 0, 16

    load("y", block(0, core, 0, 2), T.a0[:, 0:256], "la0")
    load("s", block(0, core, 2, 4), T.a0[:, 256:512], "la1")
    load("y", w("sri"), T.sr[:, :], "lsr")
    load("s", w("wti"), T.wt[:, :], "lwt")
    load("y", w("bsi", rows=8), T.bs[:, :], "lbs")

    iota(w("kc"), [[-1, 16]], 0, 1)
    iota(w("m16"), [[16, 8], [0, 16]], 0, 0)
    iota(w("lf", L_A, L_A + 16), [[1, 8], [16, 2]], 0, 0)
    iota(w("lf", L_B, L_B + 16), [[16, 2], [1, 2], [64, 4]], 0, 0)
    iota(w("num"), [[1, 160]], 0, 0)
    for a, b in OPT["send"][0]:
        send(0, a, b)
    remote([to_near(0, core, 0, 4, e_near)], [block(0, core, 0, 4)])
    forward(0)

    k = w("kc", 0, 1)
    n128 = w("num", 0, 128)
    cp(w("ki"), w("kc"))
    FIELDS = ((3, 1), (0, 7), (4, 7), (3, 3), (5, 3))
    for n, (shift, bits) in enumerate(FIELDS):
        ts(w("kj", n, n + 1), w("ki", 0, 1), shift, bits, A.arith_shift_right, A.bitwise_and)
    cp(w("rf", 0, len(FIELDS)), w("kj", 0, len(FIELDS)))
    bit3, low3, group, mid2, top2 = [w("rf", n, n + 1) for n in range(len(FIELDS))]

    def col(n, m=1):
        return w("rs", n, n + m)

    ts(col(0), bit3, 8.0, None, A.mult)
    ts(col(1), low3, 32.0, None, A.mult)
    ts(col(2), bit3, 32.0, None, A.mult)
    ts(col(3), low3, 2.0, None, A.mult)
    ts(w("lst", L_A, L_A + 16), w("lf", L_A, L_A + 16), col(0), col(1), A.add, A.add)
    ts(w("lst", L_B, L_B + 16), w("lf", L_B, L_B + 16), col(2), col(3), A.add, A.add)
    for t in range(16):
        ts(w("sel", t * 128, t * 128 + 128), w("m16"), w("kc", t, t + 1), None, A.is_equal)

    def mov(to, frm):
        a = frm * 160 + 24 - 8 * to
        return w("mov", a, a + 128)

    def fin(to, frm):
        a = frm * 160 + 3 - to
        return w("fin", a, a + 128)

    def idf(n):
        return w("idf", n * 128, n * 128 + 128)

    ts(col(12, 4), w("num", 0, 4), mid2, 1000.0, A.not_equal, A.mult)
    ts(col(16, 4), col(12, 4), k, None, A.add)
    for frm in range(4):
        ts(w("mov", frm * 160, frm * 160 + 160), w("num"), col(16 + frm), 24.0 - 8 * frm, A.subtract, A.is_equal)
    fill(w("one", rows=32), 1.0)
    for s in range(8):
        act(w("tie", s, 256, 8, rows=1), w("one", 0, 32, rows=1), scale=3.5 - s)
    ts(w("idb"), n128, k, None, A.is_equal)
    ts(w("idh"), n128, k, None, A.is_equal)
    ts(w("e8", rows=8), w("m16", rows=8), 0.0625, w("kc", 0, 1, rows=8), A.mult, A.is_equal)

    def weights(bank, chunk):
        h, c = chunk // 4, chunk % 4
        for s in range(8):
            t = 2 * s + h
            mm(w3(bank, 0, 16, s, 32, 8) if chunk in RESIDENT else w(bank, s, 512, 8),
               w("sel", t * 128, t * 128 + 128), w("wtb", c * 64, c * 64 + 64))

    def wt(c, a=0, b=512):
        if c in RESIDENT:
            return w3(RESIDENT[c], a // 32, b // 32)
        return w("wsb", IN_SBUF[c] * 512 + a, IN_SBUF[c] * 512 + b)

    cp(w("z0"), ind(w("sri"), w("lst", L_A, L_A + 16)))
    cp(w("wtb"), w("wti"))
    for c, bank in ((4, "px0"), (0, "px1"), (5, "pk0"), (1, "pk1")):
        weights(bank, c)
        act(wt(c), w(bank))
    turn(w("z1"), w("z0"))
    ts(w("zh"), ind(w("z1"), w("lst", L_B, L_B + 16)), -2048.0, None, A.add)
    for h in range(2):
        for m6 in range(2):
            for to in range(4):
                mm(w(lu[h], m6 * 64, m6 * 64 + 64), mov(to, 2 * h + m6), w("zh", to * 64, to * 64 + 64),
                   to == 0, to == 3)
        ts(w("off", h * 128, h * 128 + 128), w(lu[h], 0, 128), 2048.0, None, A.add)
    cp(w("bsh", rows=8), w("bsi", rows=8))
    weights("px0", 2)
    cp(wt(2), w("px0"))
    weights("px1", 6)
    act(wt(6), w("px1"))
    for c in RESIDENT:
        weights(RESIDENT[c], c)
    ts(col(9), low3, -4096.0, 7 * 4096.0 + 2048.0, A.mult, A.add)
    for n, c in enumerate((1.0, 1.0 / 4096, 13.0 / 4096, 7.0 / 4096)):
        act(idf(n), w("idb"), scale=c)

    def late_constants():
        ts(w("grp", 0, 8), w("num", 0, 8), group, -8.0, A.is_equal, A.mult)
        ts(w("grp", 8, 16), w("num", 0, 8), group, 8.0, A.is_equal, A.mult)
        fill(w("d1"), 0.0)
        fill(w("d1", 0, 128, 8), -3.0e7)
        fill(w("inj"), 0.0)
        fill(w("dd", 128, 4 * PAD, PAD), 0.0)
        fill(w("less", 0, 16, rows=32), 0.0)
        fill(w("less", 16, 32, rows=32), -BIG / 4096)
        fill(w("less", 32, 64, rows=32), 0.5)
        ts(w("idn"), n128, k, -4096.0, A.is_equal, A.mult)
        ts(w("idp"), n128, k, 4096.0, A.is_equal, A.mult)
        ts(col(4), low3, 4096.0, -7 * 4096.0, A.mult, A.add)
        act(w("mid", rows=1), w("tie", rows=1), scale=0.0, f=IDENT, bias=2048.0)

    def last_constants():
        ts(col(5), top2, 32.0, None, A.mult)
        ops[-1]["ext"] = landed(1)
        ts(col(6), low3, 4.0, col(5), A.mult, A.add)
        ts(col(20, 4), col(12, 4), col(6), None, A.add)
        for frm in range(4):
            ts(w("fin", frm * 160, frm * 160 + 136), w("num", 0, 136), col(20 + frm), 3.0, A.subtract, A.is_equal)

    signs = (("idn", "idp"), ("idp", "idn"))

    def put(h, blk):
        a = h * 256 + blk * 128
        return [(w("inj", a, a + 128), signs[blk][0])]

    def carried(h, blk):
        c = (2 * h + blk) * PAD
        return [(w("dd", c + 1, c + 129), signs[blk][0]), (w("dd", c, c + 128), signs[blk][1])]

    def sources(r, h):
        src = w("src", h * 128, h * 128 + 128)
        act(src, w(lu[h], 0, 128), f=IDENT, bias=0.0 if r else col(9))
        mm(w(pk[h], 256, 384), src, idf(0))
        mm(w(lu[h], 0, 128), idf(0), src, True, False)

    def choose(r, h):
        a, n = h * 256, h * 32
        src = w(pk[h], 256, 384)
        for c in OPT["kinds"]:
            scan(w("mx", a + c, a + c + 128), w("d1"), w(pk[h], c, c + 128), A.add, A.max)
        act(w("kn", n, n + 14), w("mx", a + 128 + 23, a + 256, 8), 0.125, f=IDENT, bias=BIG)
        act(w("kn", n + 14, n + 16), w("mx", a + 128 + 7, a + 128 + 16, 8), 0.125, f=IDENT, bias=BIG)
        mm(w(px[h], 0, 32), w("one", rows=1), w("less", 0, 32, rows=1), True, False)
        mm(w(px[h], 16, 32), idf(1), w("kn", n, n + 16), False, False)
        mm(w(px[h], 0, 32), w("one", rows=1), w("less", 32, 64, rows=1), False, False)
        for c in (0, 128):
            tt(w("nq", a + c, a + c + 128), w(pk[h], c, c + 128), w("mx", a + c, a + c + 128), A.not_equal)
        scan(w("sc", a, a + 128), w("nq", a, a + 128), src, A.mult, A.max)
        mm(w(px[h], 0, 16), idf(1), w("sc", a + 7, a + 128, 8), False, False)
        mm(w(px[h], 16, 32), idf(3), w("sc", a + 7, a + 128, 8), False, False)
        scan(w("sc", a + 128, a + 256), w("nq", a + 128, a + 256), src, A.mult, A.max)
        mm(w(px[h], 16, 32), idf(2), w("sc", a + 128 + 7, a + 256, 8), False, True)
        ts(w("zi", n, n + 32), w(px[h], 0, 32), 1.0 + 2.0 ** -22, None, A.mult)
        tt(w("inj", a + 7, a + 256, 8), w(px[h], 0, 32), w("zi", n, n + 32), A.subtract)
        for x, sign in put(h, 0) + put(h, 1):
            mm(w(lu[h], 0, 128), x, w(sign), False, False)
        for blk in range(2):
            c = (2 * h + blk) * PAD
            scan(w("dd", c, c + 128, -1), w("inj", a + blk * 128, a + blk * 128 + 128, -1),
                 w("nq", a, a + 128, -1), A.add, A.mult)
            for m, (x, sign) in enumerate(carried(h, blk)):
                mm(w(lu[h], 0, 128), x, w(sign), False, blk == 1 and m == 1)
        if r < RO - 1:
            ts(w("off", h * 128, h * 128 + 128), w(lu[h], 0, 128), col(4), None, A.add)

    def unlist(h):
        ts(w("zh", h * 128, h * 128 + 128), w(lu[h], 0, 128), col(4), -2048.0, A.add, A.add)
        for m6 in range(2):
            for frm in range(4):
                c = frm // 2 * 16
                mm(w3("pw0", 0, 8, c + frm % 2, c + 16, 2), fin(2 * h + m6, frm),
                   w("zh", h * 128 + m6 * 64, h * 128 + m6 * 64 + 64), False, (h, m6, frm) == (1, 1, 3))

    for r in range(RO):
        last = r == RO - 1
        tab = w("tab%d" % r)
        arrived = landed(r)

        def new_a(a, b):
            return w("aout", a * 128, b * 128) if last else block(r + 1, core, a, b)

        def sums(qt, a=0, b=128):
            return w(pk[qt // 2], 384 + a, 384 + b) if qt % 2 else w(px[qt // 2], a, b)

        def picked(c, a, b):
            return ind(tab, w("off", c * 32 + a // 16, c * 32 + b // 16))

        def gather(c, a, b):
            act(w("p", c * 512 + a, c * 512 + b), picked(c, a, b), ext=arrived)

        def gather_mul(c, a, b):
            tt(w("wp", c * 512 + a, c * 512 + b), picked(c, a, b), wt(c, a, b), A.mult, ext=arrived)

        def mul(c, a, b):
            tt(w("wp", c * 512 + a, c * 512 + b), w("p", c * 512 + a, c * 512 + b), wt(c, a, b), A.mult)

        def wires(c):
            a = c % 2 * 64
            for s in range(8):
                mm(sums(c // 2, a, a + 64), w("idh"), w("wp", c * 512 + s, c * 512 + 512, 8),
                   False, c % 2 == 1 and s == 7)

        def clamp(qt):
            if qt in OPT["clamp_s"]:
                act(w("neg", qt * 128, qt * 128 + 128), sums(qt), -1.0, f=RELU, bias=255.0)
                act(new_a(qt, qt + 1), w("neg", qt * 128, qt * 128 + 128), -1.0, f=RELU, bias=255.0)
            else:
                ts(new_a(qt, qt + 1), sums(qt), 0.0, 255.0, A.max, A.min)
            if last and qt % 2:
                store("y", T.ya[:, qt // 2 * 256:qt // 2 * 256 + 256], new_a(qt - 1, qt + 1), "oy%d" % (qt // 2))
            for a, b in () if last else OPT["send"][r + 1]:
                if b == qt + 1:
                    send(r + 1, a, b)
            c = 256 + qt % 2 * 128
            mm(w(px[qt // 2], c, c + 128), w("idb"), new_a(qt, qt + 1))

        def score(h, s):
            a = (h * 8 + s) * 256
            tt(w("q", a, a + 256), w("p", h * 2048 + s, h * 2048 + 2048, 8), w(px[h], 256, 512), A.mult)
            for b in range(2):
                mm(w(pk[h], b * 8 + s, 256, 16), w("q", a + b, a + 256, 2), w("grp"), False, s == 7 and b == 1)

        def again(h):
            for c in OPT["fused"][r]:
                if c // 4 == h:
                    gather(c, 0, 256)
                    gather(c, 256, 512)

        for qt in range(4):
            if qt % 2:
                sources(r, qt // 2)
            mm(sums(qt), w("e8", rows=8), w("bsh", qt * 128, qt * 128 + 128, rows=8), True, False)
            for c in range(2 * qt, 2 * qt + 2):
                for a, b in OPT["pieces"].get(c, ((0, 512),)):
                    if c in OPT["fused"][r]:
                        gather_mul(c, a, b)
                    else:
                        hold[0] = OPT["hold_mul"][r]
                        gather(c, a, b)
                        mul(c, a, b)
                        hold[0] = {}
                wires(c)
            hold[0] = OPT["hold_clamp"]
            clamp(qt)
            hold[0] = {}
            if qt == 1 and OPT["again"]:
                again(0)
        if not OPT["again"]:
            again(0)
        again(1)
        if not last:
            forward(r + 1)
        if r == 0:
            late_constants()
        for h in range(2):
            mm(w(pk[h], 0, 256), w("one", rows=1), w("tie", rows=1), True, False)
            for s in range(8):
                if last and h == 1 and s == OPT["late"]:
                    choose(r, 0)
                score(h, s)
            if not last:
                hold[0] = OPT["hold_steps"][h]
                choose(r, h)
                hold[0] = {}
        if r == 1:
            last_constants()
        if last:
            mm(w3("pw0", 0, 8), w("one", rows=1), w("mid", rows=1), True, False)
            hold[0] = OPT["hold_last"]
            choose(r, 1)
            hold[0] = {}
            if OPT["late"] == 8:
                choose(r, 0)
            for h in range(2):
                unlist(h)
    for x in range(8):
        turn(w("z0", x, 256, 8), w3("pw0", x, x + 1))
    store("y", T.ys[:, :], w("z0"), "oys")

    def arrange(ops):
        WAKE, DMA = OPT["wake"], 2700
        before = [dict() for _ in ops]
        seen, last_send, last_of = {}, {}, {}
        for n, o in enumerate(ops):
            for views, writing in ((o["r"], False), (o["w"], True)):
                for name, _, bits in views:
                    for m, mbits, mw in seen.get(name, []):
                        if (psum(name) and (mw or writing or ops[m]["q"] != o["q"])
                                or (mw or writing) and mbits & bits and not ops[m]["mute"]):
                            both_t = ops[m]["q"] == "t" and o["q"] == "t"
                            before[n][m] = DMA if ops[m]["dma"] else 0 if both_t else WAKE
            for views, writing in ((o["r"], False), (o["w"], True)):
                for name, _, bits in views:
                    seen.setdefault(name, []).append((n, bits, writing))
            if o["dma"]:
                if o["q"] in last_of:
                    before[n].setdefault(last_of[o["q"]], 0)
                last_of[o["q"]] = n
            for name, _ in o["ext"]:
                before[n][last_send[name]] = OPT["land"][name[:-1]] / 0.83e-3
            if "sends" in o:
                last_send[o["sends"]] = n
        after = [[] for _ in ops]
        for n, b in enumerate(before):
            for m in b:
                after[m].append(n)
        waiting = [len(b) for b in before]
        ready = {q: [n for n, o in enumerate(ops) if o["q"] == q and not waiting[n]] for q in queue}
        can = [0.0] * len(ops)
        free = {q: 0.0 for q in queue}
        order = []
        while len(order) < len(ops):
            q = min((q for q in queue if ready[q]), key=lambda q: max(free[q], min(can[n] for n in ready[q])))
            now = max(free[q], min(can[n] for n in ready[q]))
            n = min(n for n in ready[q] if can[n] <= now + ops[n]["hold"])
            ready[q].remove(n)
            order.append(n)
            free[q] = max(now, can[n]) + ops[n]["cost"]
            for m in after[n]:
                can[m] = max(can[m], free[q] + before[m][n])
                waiting[m] -= 1
                if not waiting[m]:
                    ready[ops[m]["q"]].append(m)
        return [ops[n] for n in order]

    ops = arrange(ops)

    history = {}
    for n, o in enumerate(ops):
        deps = set()
        for views, writing in ((o["r"], False), (o["w"], True)):
            for name, _, bits in views:
                seen = set()
                for m, mq, mbits, mw in reversed(history.get(name, [])):
                    if mq == o["q"] and ops[m]["dma"] is None:
                        hit = mq != "t" and (mbits & bits) and (mw or writing)
                    else:
                        hit = psum(name) or ((mbits & bits) and (mw or writing))
                    key = ops[m]["dma"] or mq
                    if hit and not ops[m]["mute"] and key not in seen:
                        seen.add(key)
                        deps.add(m)
        o["deps"] = deps
        for views, writing in ((o["r"], False), (o["w"], True)):
            for name, _, bits in views:
                history.setdefault(name, []).append((n, o["q"], bits, writing))

    known = {q: {} for q in queue}
    for n, o in enumerate(ops):
        need = {}
        for m in o["deps"]:
            key = ops[m]["dma"] or ops[m]["q"]
            if known[o["q"]].get(key, -1) < m:
                need[key] = max(need.get(key, -1), m)
        for key, m in need.items():
            known[o["q"]][key] = m
            ops[m]["signal"] = True
        o["need"] = sorted(need.values())

    done = {q: 0 for q in queue}
    waited = {q: set() for q in queue}
    for o in ops:
        q = o["q"]
        for m in o["need"]:
            queue[q].wait_ge(T.sem[ops[m]["token"][0]], ops[m]["token"][1])
        for e in o["ext"]:
            if e not in waited[q]:
                waited[q].add(e)
                queue[q].wait_ge(T.sem[e[0]], e[1])
        ins = o["fn"]()
        if o["dma"]:
            ins.then_inc(T.sem[o["dma"]], 16)
            o["token"] = (o["dma"], 16)
        elif o.get("signal"):
            done[q] += 1
            ins.then_inc(T.sem[own_sem[q]], 1)
            o["token"] = (own_sem[q], done[q])
    g.wait_ge(T.sem.sent, sent[0])
    for name in ("oy0", "oy1", "oys"):
        g.sync.wait_ge(T.sem[name], 16)
